import numpy as np, ml_dtypes
CORES = [35,38,43,46]
N = 4
import mx_ref
BF = ml_dtypes.bfloat16
def entries(a):
    return np.ascontiguousarray(a.T).reshape(-1)
def table(e):
    return np.ascontiguousarray(np.reshape(e, (-1, 16)).T).astype(np.int32)
def cols(t, e):
    v = np.concatenate([t.reshape(128, -1, 4), np.zeros((128, 1, 4), BF)], axis=1)
    return np.ascontiguousarray(v[:, e]).reshape(128, -1)
def f(rng, *shape):
    return mx_ref.flush((rng.standard_normal(shape, dtype=np.float32) * np.exp2(rng.integers(-2, 3, shape[:-1] + (1,)))).astype(BF))
def wide(rng, *shape, cols=0):
    v = rng.standard_normal(shape, dtype=np.float32) * np.exp2(rng.integers(-12, 13, shape)).astype(np.float32)
    if cols: v *= np.repeat(np.exp2(rng.integers(-cols, cols + 1, shape[:-2] + (1, shape[-1] // 4))) * (rng.random(shape[:-2] + (1, shape[-1] // 4)) > 0.0625), 4, axis=-1).astype(np.float32)
    return mx_ref.flush(v.astype(BF))
T, S, O, CAPP = 512, 768, 2, (256, 480)
B = len(CAPP)
def wanters(q, b):
    return sum(1 << e for e in range(N) if (e ^ q ^ (1 << b)) % (2 << b) == 0)
def holders(q, b):
    return (q >> b) << b, ((q >> b) + 1) << b
def limit(rng, m, keep, lo, hi, s, most):
    v = m.reshape(-1)
    e = np.flatnonzero(v[lo * T:hi * T] & s) + lo * T
    e = e[np.argsort(rng.random(len(e)) - ((keep.reshape(-1)[e] & s) != 0))][most:]
    v[e] &= ~s
def masks(rng, keep=None, off=None, share=0.55):
    keep = np.zeros((N, T), int) if keep is None else keep
    off = np.zeros((N, T), bool) if off is None else off
    for r in range(N):
        if not ((keep >> r) & 1).any(): keep[r, rng.choice(np.flatnonzero(~off[r]))] |= 1 << r
    n = rng.integers(1, 4, (N, T)) * (rng.random((N, T)) < share)
    m = ((np.argsort(rng.random((N, T, N)), axis=2) < n[:, :, None]) * (1 << np.arange(N))).sum(axis=2)
    m = np.ascontiguousarray(np.where(off, 0, m) | keep)
    for b in range(B):
        for q in range(N): limit(rng, m, keep, *holders(q, b), wanters(q, b), CAPP[b])
    for r in range(N): limit(rng, m, keep, 0, N, 1 << r, S)
    return {"dm": np.stack([table(v) for v in m])}
def setup_inputs(rng):
    return {"x": f(rng, N, 128, 4 * T), **masks(rng), "w": f(rng, N, 128, 512 * O)}
def setup_inputs_comb(rng):
    k = np.zeros((N, T), int); c = np.arange(T); s = int(rng.integers(0, 16)); p = int(rng.integers(0, N)); g = p ^ (N >> 1)
    for e in range(N): k[:, (c - e - s) % 4 == 0] |= 1 << e
    lo, hi = holders(p, B - 1)
    k[lo:hi] &= ~(1 << g)
    k[p, c % 16 != s] |= 1 << g
    assert not check_inputs({"dm": np.stack([table(v) for v in k])})
    return {**setup_inputs(rng), **masks(rng, k)}
def setup_inputs_turn(rng):
    k = np.zeros((N, T), int); g = int(rng.integers(0, N))
    k[g ^ 1, rng.permutation(T)[:CAPP[0]]] |= 1 << g
    k[g ^ 3, rng.permutation(T)[:CAPP[0]]] |= 1 << g
    h = rng.permutation(T)
    k[g, h[:CAPP[0]]] |= 1 << (g ^ 3)
    k[g, h[CAPP[0]:2 * CAPP[0]]] |= 1 << (g ^ 2)
    if N == 8: k[g ^ 6, rng.permutation(T)[:CAPP[1]]] |= 1 << (g ^ 4)
    return {**setup_inputs(rng), **masks(rng, k)}
def setup_inputs_none(rng):
    z = np.zeros((N, T), bool); k = np.zeros((N, T), int); p = int(rng.integers(0, N))
    for r in range(N): z[r, rng.permutation(T)[:T // 2]] = True
    k[p ^ 1, rng.choice(np.flatnonzero(~z[p ^ 1]))] |= 1 << p
    d = {**setup_inputs(rng), **masks(rng, k, off=z, share=1)}
    d["dm"][p] = 0
    return d
def setup_inputs_full(rng):
    k = np.zeros((N, T), int); g = int(rng.integers(0, N)); s = int(rng.integers(0, T))
    k[g ^ 1, (np.arange(CAPP[0]) + s) % T] |= 1 << (g ^ 2)
    k[g, (np.arange(S - sum(CAPP[1:])) + s) % T] |= 1 << g
    for b in range(1, B):
        for r in range(N):
            if r >> b == (g >> b) ^ 1: k[r, (np.arange(CAPP[b] >> b) + s) % T] |= 1 << g
    assert not check_inputs({"dm": np.stack([table(v) for v in k])})
    return {**setup_inputs(rng), **masks(rng, k, share=1)}
def setup_inputs_spread(rng):
    d = setup_inputs(rng); d["x"] = wide(rng, N, 128, 4 * T, cols=8); return d
def check_inputs(d):
    bad = []
    m = np.stack([entries(v) for v in d["dm"]]).astype(np.int64)
    if m.min() < 0 or m.max() >= 1 << N: bad.append("dm")
    for r in range(N):
        if ((m >> r) & 1).sum() > S: bad.append("arrivals")
    for b in range(B):
        for q in range(N):
            lo, hi = holders(q, b)
            if ((m[lo:hi] & wanters(q, b)) != 0).sum() > CAPP[b]: bad.append("CAPP_" + str(b))
    return bad
def reference(x, dm, w):
    m = np.stack([entries(v) for v in dm])
    every = np.concatenate(list(x), axis=1)
    y = np.zeros((N, 128, O * S), np.float32); ln = np.zeros((N, 1, 2), np.float32)
    for r in range(N):
        e = np.flatnonzero((m.reshape(-1) >> r) & 1); n = len(e)
        k = np.full(S, -1); k[:n] = e
        a = mx_ref.quantize(cols(every, k))
        for o in range(O):
            y[r][:, S * o:S * o + n] = mx_ref.matmul(mx_ref.quantize(np.ascontiguousarray(w[r][:, 512 * o:512 * o + 512])), a)[:, :n]
        ln[r, 0, 0] = n; ln[r, 0, 1] = np.count_nonzero((m[r] >> r) & 1)
    return {"y": y, "ln": ln}

@@ -1,0 +1,403 @@
+import numpy as np
+from concourse.bass import DstId, RemoteDMATransfer
+from concourse.mybir import dt, AluOpType, AxisListType, ActivationFunctionType
+
+T_, S_, C0, C1 = 512, 768, 256, 480
+EARLY = C1 - C0
+OWN = T_ - EARLY
+FB = T_ + C0
+RW = FB + C1 + 32
+ZC = FB + C1
+CUTS = (0, 128, 384, 768)
+FAR = 16 * 127 + 16
+LS = 256.0 + C0 - EARLY
+NONE = 4096.0
+BIG = 8192.0
+
+F32, I32, U16, BF = "float32", "int32", "uint16", "bfloat16"
+Q4, U8 = "float8_e4m3fn_x4", "uint8"
+
+
+def sb(n, d):
+    return ("sbuf", [128, n], d)
+
+
+SCRATCH = {
+    "dmt": sb(68, I32),
+    "xt": sb(2048, BF), "wt": sb(1024, BF),
+    "xq": sb(512, Q4), "xs": sb(512, U8), "wq": sb(256, Q4), "ws": sb(256, U8),
+    "xwq": sb(C0 + OWN, Q4), "xws": sb(C0 + OWN, U8),
+    "p0q": sb(256, Q4), "p0s": sb(256, U8),
+    "peq": sb(EARLY, Q4), "pes": sb(EARLY, U8), "plq": sb(256, Q4), "pls": sb(256, U8),
+    "leq": sb(EARLY, Q4), "les": sb(EARLY, U8), "llq": sb(256, Q4), "lls": sb(256, U8),
+    "one": sb(32, F32), "half": sb(32, F32), "hpm": sb(32, F32), "cb": sb(1, F32), "sgn": sb(1, F32),
+    "ho": sb(1, F32), "hf": sb(1, F32),
+    "pi": sb(2, I32), "pint": sb(8, I32), "pf": sb(8, F32),
+    "val0": sb(256, BF), "valb": sb(256, BF), "dd0": sb(32, F32), "dd": sb(32, F32), "i480": sb(64, F32), "i48": sb(64, F32),
+    "dfl": sb(16, F32),
+    "ta": sb(16, I32), "tb": sb(16, I32), "td": sb(32, I32),
+    "z0": sb(96, F32), "zt0": sb(64, F32), "car0": sb(1, F32), "pt0": sb(32, F32), "zb0": sb(32, F32), "m0": sb(32, F32),
+    "a0": sb(32, F32), "h0": sb(32, F32), "hm": sb(32, F32), "o0": sb(16, U16), "slt": sb(32, F32),
+    "z3": sb(96, F32), "zt3": sb(64, F32), "car3": sb(1, F32), "pt3": sb(32, F32), "zb3": sb(32, F32), "m3": sb(32, F32),
+    "x3": sb(32, F32), "w3": sb(32, F32), "y3": sb(32, F32), "a3": sb(32, F32), "h3": sb(32, F32), "o3": sb(16, U16),
+    "winu": sb(1024 + FAR, BF), "tu": sb(960, BF), "yu": sb(128, F32), "ytu": sb(128, F32), "yuu": sb(64, F32),
+    "off0": sb(16, U16), "offu": sb(14, U16),
+    "winf": sb(1024 + FAR, BF), "tf": sb(S_, BF), "yf": sb(64, F32), "ytf": sb(64, F32), "yff": sb(64, F32), "sw": sb(64, F32),
+    "slu": sb(32, BF), "slin": sb(32, BF),
+    "rexp": sb(32, F32), "ct": sb(32, F32), "cuv": sb(8, F32), "rexp3": sb(32, F32), "ct3": sb(32, F32),
+    "cf": sb(4, F32), "cg": sb(4, F32),
+    "lc": sb(16, F32), "offl": sb(16, U16),
+    "sc": sb(16, F32), "lnt": sb(2, F32),
+    "tl": sb(64, F32), "la": sb(64, F32), "wa": sb(64, F32), "lb": sb(64, F32), "wb": sb(64, F32),
+    "ma": sb(64, F32), "mb": sb(64, F32), "fm": sb(64, F32), "fh": sb(64, F32), "fl": sb(64, F32), "fl2": sb(64, F32),
+    "offf": sb(64, U16),
+    "res0": sb(RW, F32), "res1": sb(RW, F32), "yt_0": sb(768, F32), "yt_1": sb(768, F32),
+    "ps": ("psum", [128, 4096], F32),
+}
+SEMAPHORES = ["sv", "sa", "st", "sg", "dml", "xl0", "xl1", "wl", "xw", "vps", "yst",
+              "aDM", "aS0", "aSL", "aCNT", "aE", "aL", "loc"]
+
+
+def rank_program(g, core, T, topo):
+    q = T.rank_of(core)
+    if q is None:
+        return
+    A = AluOpType
+    AF = ActivationFunctionType
+    X = AxisListType.X
+    rp, rf, rg = q ^ 1, q ^ 2, q ^ 3
+    cp, cf_, cg_ = T.cores[rp], T.cores[rf], T.cores[rg]
+    P, Fb, G, Qb = 1 << rp, 1 << rf, 1 << rg, 1 << q
+    s = T.sem
+    cnt = {"sv": 0, "sa": 0, "st": 0, "loc": 0}
+    seen = {}
+    L, U = slice(0, 64), slice(64, 128)
+
+    def wait(name, eng, sem, n):
+        if n > 0 and seen.get((name, sem), 0) < n:
+            seen[(name, sem)] = n
+            eng.wait_ge(s[sem], n)
+
+    def V(ins, d=0):
+        wait("v", g.vector, "sv", d)
+        r = ins()
+        cnt["sv"] += 1
+        r.then_inc(s.sv, 1)
+        return cnt["sv"]
+
+    def SA(ins, v=0, a=0):
+        wait("a", g.scalar, "sv", v)
+        wait("a", g.scalar, "sa", a)
+        r = ins()
+        cnt["sa"] += 1
+        r.then_inc(s.sa, 1)
+        return cnt["sa"]
+
+    def vsa(n):
+        wait("v", g.vector, "sa", n)
+
+    def ts(out, in0, s1, s2, op0, op1=None, d=0):
+        if op1 is None:
+            return V(lambda: g.vector.tensor_scalar(out, in0, s1, s2, op0), d)
+        return V(lambda: g.vector.tensor_scalar(out, in0, s1, s2, op0, op1), d)
+
+    def tt(out, a, b, op, d=0):
+        return V(lambda: g.vector.tensor_tensor(out, a, b, op), d)
+
+    def cpy(out, in_, d=0):
+        return V(lambda: g.vector.tensor_copy(out, in_), d)
+
+    def tr(out, in_, d=0):
+        return V(lambda: g.vector.transpose(out, in_), d)
+
+    def red(out, in_, d=0):
+        return V(lambda: g.vector.tensor_reduce(out, in_, X, A.add), d)
+
+    def scan(out, d1, init, d=0):
+        return V(lambda: g.vector.tensor_tensor_scan(out, T.one[:], d1, init, A.mult, A.add), d)
+
+    def fill(ap, c, d=0):
+        return V(lambda: g.vector.memset(ap, c), d)
+
+    def act(out, in_, v=0, a=0, f=AF.Copy, scale=None, bias=None):
+        kw = {}
+        if scale is not None:
+            kw["scale"] = scale
+        if bias is not None:
+            kw["bias"] = bias
+        return SA(lambda: g.scalar.activation(out, in_, f, **kw), v, a)
+
+    def send(dst, out, in_, rsem):
+        rid, pid, _se = topo.addr(dst)
+        g.remote_dma(out_ap=out, in_ap=in_, remote_sem=s[rsem], local_sem=s.loc, pid=pid, routing_id=rid,
+                     dma_engine_mask=topo.mask(core, dst))
+        cnt["loc"] += len(topo.engines(core, dst))
+
+    ncp, nmf = len(topo.engines(core, cp)), len(topo.engines(core, cf_))
+
+    def b8(ap):
+        return ap.bitcast(dt.uint8)
+
+    def b32(ap):
+        return ap.bitcast(dt.uint32)
+
+    even = q < rp
+    ob = 4 if even else 36
+    for k in range(8):
+        e = g.sync if k % 2 == 0 else g.scalar
+        o = ob - k % 2
+        e.dma_start(T.dmt[16 * k:16 * k + 16, o:o + 32], T.dm[:, :]).then_inc(s.dml, 16)
+    g.sync.dma_start(T.xt[:, 4 * EARLY:2048], T.x[:, 4 * EARLY:2048]).then_inc(s.xl0, 16)
+    g.scalar.dma_start(T.xt[:, 0:4 * EARLY], T.x[:, 0:4 * EARLY]).then_inc(s.xl1, 16)
+    g.scalar.dma_start(T.wt[:], T.w[:]).then_inc(s.wl, 16)
+
+    FL = {"allow_small_or_imprecise_dtypes": True}
+    g.iota(T.pi[:, 0:1], [[1, 1]], 0, 1).then_inc(s.sg, 1)
+    g.iota(T.val0[:], [[32, 16], [1, 16]], -256, 0, **FL).then_inc(s.sg, 1)
+    g.iota(T.dd0[:], [[0, 2], [16, 16]], 1024, 0, **FL).then_inc(s.sg, 1)
+    g.iota(T.i480[:], [[S_ // 2, 2], [16, 32]], 0, 0, **FL).then_inc(s.sg, 1)
+    g.wait_ge(s.dml, 128)
+    send(cp, T.dmt[:, ob:ob + 31], T.dmt[:, ob:ob + 31], "aDM")
+    g.iota(T.yu[:], [[0, 128]], 0, 0, **FL).then_inc(s.sg, 1)
+
+    nwu = fill(T.winu[:, 0:512], -NONE)
+    g.vector.wait_ge(s.sg, 1)
+    ts(T.pint[:, 0:1], T.pi[:, 0:1], 16, None, A.bitwise_and)
+    n = ts(T.pint[:, 1:2], T.pi[:, 0:1], 15, None, A.bitwise_and)
+    fill(T.one[:], 1.0)
+    fill(T.z0[L, 31:32], C0 / 16.0)
+    npf = cpy(T.pf[:, 0:2], T.pint[:, 0:2], n)
+    fill(T.z0[U, 31:32], -2.0 / 32)
+    fill(T.z0[U, 48:64], 0.0)
+    fill(T.sgn[L, :], -2.0)
+    nsgn = fill(T.sgn[U, :], 2.0)
+    g.vector.wait_ge(s.sg, 2)
+    ts(T.valb[:], T.val0[:], T.pf[:, 0:1], None, A.add, d=npf)
+
+    act(T.winu[:, 512:960], T.winu[:, 0:448], nwu)
+    nwf0 = act(T.winf[:, 0:512], T.winu[:, 0:512], scale=-1.0)
+
+    g.vector.wait_ge(s.dml, 128)
+    ts(T.ta[L, :], T.dmt[L, ob:ob + 31:2], G, None, A.bitwise_and)
+    na = ts(T.ta[U, :], T.dmt[U, ob:ob + 31:2], Fb, None, A.bitwise_and)
+    nb = ts(T.tb[L, :], T.dmt[L, ob:ob + 31:2], P | G, None, A.bitwise_and)
+    fill(T.hpm[L, :], -0.5)
+    ts(T.z0[:, 32:48], T.ta[:], 0.0, T.sgn[:], A.is_gt, A.mult, d=max(na, nsgn))
+    nz = ts(T.z0[L, 48:64], T.tb[L, :], float(P), -2.0, A.is_equal, A.mult, d=nb)
+    fill(T.hpm[U, :], 0.5)
+    fill(T.cb[L, :], float(C0))
+    n = scan(T.z0[:, 64:96], T.z0[:, 31:63], 0.0, nz)
+    nzb = ts(T.zb0[:], T.z0[:, 32:64], 0.0, 65536.0, A.not_equal, A.mult)
+    g.vector.wait_ge(s.sg, 3)
+    ndd = ts(T.dd[:], T.dd0[:], T.pf[:, 1:2], None, A.add)
+    n = tr(T.zt0[:], T.z0[:, 32:96], n)
+    fill(T.cb[U, :], 1.0)
+    fill(T.hm[:], 0.0)
+    n = red(T.car0[:], T.zt0[:, 32:64], n)
+    nm = tt(T.m0[:], T.dd[:], T.zb0[:], A.subtract, max(nzb, ndd))
+    fill(T.half[:], 0.5)
+    np0 = scan(T.pt0[:], T.zt0[:, 0:32], T.car0[:], n)
+    fill(T.z3[:, 31:32], -2.0 / 32)
+    fill(T.ho[L, :], 256.0)
+    n = tr(T.h0[:], T.pt0[:], np0)
+    nrx = ts(T.rexp[:], T.hpm[:], T.pt0[:, 31:32], T.cb[:], A.mult, A.add)
+    fill(T.ho[U, :], 512.0)
+    n = tt(T.a0[:], T.h0[:], T.m0[:], A.max, max(n, nm))
+    nct = tr(T.ct[:], T.rexp[:], nrx)
+    fill(T.hf[L, :], FB - 256.0)
+    n = tt(T.hm[:, 0:16], T.a0[:, 0:16], T.a0[:, 16:32], A.min, n)
+    fill(T.hf[U, :], FB - 512.0)
+    g.vector.wait_ge(s.sg, 4)
+    ni48 = ts(T.i48[:], T.i480[:], T.pf[:, 1:2], None, A.add)
+    n = cpy(T.o0[:], T.hm[:, 0:16], n)
+    nslt = tr(T.slt[:], T.hm[:])
+    vsa(nwf0)
+    nwin = cpy(T.winu[:].indirect(T.o0[:]), T.valb[:], n)
+    act(T.cuv[L, 0:4], T.ct[L, 15:19], nct)
+    nslu = act(T.slu[:], T.slt[:], nslt, scale=0.5)
+    act(T.cuv[U, 0:4], T.ct[L, 15:19])
+    act(T.cuv[L, 4:8], T.ct[U, 15:19])
+    ncuv = act(T.cuv[U, 4:8], T.ct[U, 15:19])
+    nwf = act(T.winf[:, 512:S_], T.winf[:, 0:S_ - 512], 0, nwf0)
+    g.vector.wait_ge(s.xl0, 16)
+    nxq0 = V(lambda: g.vector.quantize_mx(T.xq[:, EARLY:T_], T.xs[:, EARLY:T_], T.xt[:, 4 * EARLY:2048]))
+    n = tr(T.tu[:, 0:512], T.winu[:, 0:512], nwin)
+    ndfl = ts(T.dfl[:], T.i48[:, 0:16], -LS, None, A.add, d=ni48)
+    g.vector.wait_ge(s.aDM, ncp)
+    n3 = ts(T.td[:], T.dmt[:, 4:67:2], Qb, None, A.bitwise_and)
+    g.vector.wait_ge(s.sg, 5)
+    tt(T.yu[:, 0:16], T.tu[:, 0:512:32], T.tu[:, 16:512:32], A.max, n)
+    n = tt(T.yu[:, 32:48], T.tu[:, 0:512:32], T.tu[:, 16:512:32], A.max)
+    n3 = ts(T.z3[:, 32:64], T.td[:], 0.0, 2.0, A.is_gt, A.mult, d=n3)
+    n = tr(T.ytu[:, 0:64], T.yu[:, 0:64], n)
+    n3 = scan(T.z3[:, 64:96], T.z3[:, 31:63], 0.0, n3)
+    ny = tr(T.yuu[:, 0:32], T.ytu[:, 0:64:2], n)
+    g.vector.wait_ge(s.xl1, 16)
+    V(lambda: g.vector.quantize_mx(T.xq[:, 0:EARLY], T.xs[:, 0:EARLY], T.xt[:, 0:4 * EARLY]))
+    ts(T.off0[L, :], T.yuu[L, 0:16], 256.0, None, A.add, d=ny)
+    noff0 = ts(T.off0[U, :], T.yuu[L, 0:16], 256.0, None, A.add)
+    ts(T.offu[L, :], T.yuu[U, 0:14], 256.0, None, A.add)
+    n3 = tr(T.zt3[:], T.z3[:, 32:96], n3)
+    nq0 = cpy(b32(T.p0q[:]), b32(T.xq[:]).indirect(T.off0[:]), noff0)
+    na0 = SA(lambda: g.scalar.activation(T.p0s[:], T.xs[:].indirect(T.off0[:]), AF.Copy), noff0)
+    noffu = ts(T.offu[U, :], T.yuu[U, 0:14], 256.0, None, A.add)
+    n3 = red(T.car3[:], T.zt3[:, 32:64], n3)
+    nzb = ts(T.zb3[:], T.z3[:, 32:64], 0.0, 65536.0, A.not_equal, A.mult)
+    npe = cpy(b32(T.peq[:]), b32(T.xq[:]).indirect(T.offu[:]), noffu)
+    nae = SA(lambda: g.scalar.activation(T.pes[:], T.xs[:].indirect(T.offu[:]), AF.Copy), noffu)
+
+    wait("s", g.sync, "sv", nxq0)
+    g.sync.dma_start(b8(T.xwq[:, C0:C0 + OWN]), b8(T.xq[:, EARLY:T_])).then_inc(s.xw, 16)
+    g.sync.dma_start(T.xws[:, C0:C0 + OWN], T.xs[:, EARLY:T_]).then_inc(s.xw, 16)
+    g.sync.wait_ge(s.aSL, ncp)
+    for k in range(4, 8):
+        h = k % 2
+        g.sync.dma_start(T.valb[16 * k:16 * k + 1, :], T.slin[0:16, 16 * h:16 * h + 16]).then_inc(s.vps, 16)
+
+    wait("g", g, "sa", nslu)
+    send(cp, T.slin[:], T.slu[:], "aSL")
+    wait("g", g, "sa", ncuv)
+    trs = []
+    for dst, land, c, h in ((cf_, T.cf, 4, 0), (cg_, T.cg, 0, 1)):
+        en = topo.engines(core, dst)
+        en = en[:len(en) // 2] if h == 0 else en[len(en) // 2:]
+        rid, pid, _se = topo.addr(dst)
+        trs.append(RemoteDMATransfer(dst_ids=[DstId(rid=rid, pnc=pid)], dma_engine_mask=sum(1 << e for e in en),
+                                     remote_sem=s.aCNT, src=T.cuv[:, c:c + 4], dst=land[:]))
+        cnt["loc"] += len(en)
+    g.remote_dma_fused(trs, local_sem=s.loc)
+    for b, a, n in ((T.yf, 0, 64), (T.res0, ZC, 32), (T.res1, ZC, 32)):
+        g.iota(b[:, a:a + n], [[0, n]], 0, 0, **FL).then_inc(s.sg, 1)
+    wait("g", g, "sv", nq0)
+    send(cp, b8(T.xwq[:, 0:C0]), b8(T.p0q[:]), "aS0")
+    wait("g", g, "sa", na0)
+    send(cp, T.xws[:, 0:C0], T.p0s[:], "aS0")
+    wait("g", g, "sv", npe)
+    send(cf_, b8(T.leq[:]), b8(T.peq[:]), "aE")
+    wait("g", g, "sa", nae)
+    send(cf_, T.les[:], T.pes[:], "aE")
+
+    local_first = q < rf
+    u, v = T.cf[:, 0:1], T.cg[:, 0:1]
+    nf2, ba = T.sc[:, 0:1], T.sc[:, 1:2]
+    fline = rf < rg
+    nl, fst = T.ct3[:, 31:32], T.ct3[:, 15:16]
+    na_, nq = T.lnt[:, 0:1], T.lnt[:, 1:2]
+    lo, hi = (slice(0, 16), slice(16, 32)) if even else (slice(16, 32), slice(0, 16))
+    first, second = (u, v) if fline else (v, u)
+    t = T.tl[:]
+    x3 = T.pt3 if local_first else T.x3
+    nu = tr(T.tu[:, 512:960], T.winu[:, 512:960], nwin)
+    npt = np3 = scan(T.pt3[:], T.zt3[:, 0:32], T.car3[:], n3)
+    nm3 = tt(T.m3[:], T.dd[:], T.zb3[:], A.subtract, nzb)
+    tt(T.yu[:, 64:80], T.tu[:, 448:960:32], T.tu[:, 464:960:32], A.max, nu)
+    nu = tt(T.yu[:, 96:112], T.tu[:, 448:960:32], T.tu[:, 464:960:32], A.max)
+    nrx3 = ts(T.rexp3[:], T.half[:], T.pt3[:, 31:32], 1.0, A.mult, A.add, d=npt)
+    g.vector.wait_ge(s.aCNT, nmf)
+    if not local_first:
+        n = ts(nf2, u, v, 2.0, A.add, A.mult)
+    nba = 0 if fline else ts(ba, v, -1.0, C1 - 1.0, A.mult, A.add)
+    nu = tr(T.ytu[:, 64:128], T.yu[:, 64:128], nu)
+    if not local_first:
+        np3 = ts(T.x3[:], T.pt3[:], nf2, None, A.add, d=n)
+    g.vector.wait_ge(s.wl, 16)
+    nwq = V(lambda: g.vector.quantize_mx(T.wq[:], T.ws[:], T.wt[:]))
+    nu = tr(T.yuu[:, 32:64], T.ytu[:, 64:128:2], nu)
+    n3 = ts(T.w3[:], x3[:], float(S_), 1.0 - S_, A.is_ge, A.mult, d=np3)
+    nc3 = tr(T.ct3[:], T.rexp3[:], nrx3)
+    nc = tt(T.lc[U, :], T.dfl[U, :], T.yuu[U, 32:48], A.max, max(nu, ndfl))
+    n3 = tt(T.y3[:], x3[:], T.w3[:], A.add, n3)
+    if local_first:
+        nt = ts(t, T.i48[:], nl, first, A.subtract, A.subtract, d=nc3)
+    else:
+        nt = ts(t, T.i48[:], first, None, A.subtract)
+    ts(T.offl[L, :], T.lc[U, :], LS, None, A.add, d=nc)
+    noffl = ts(T.offl[U, :], T.lc[U, :], LS, None, A.add)
+    n3 = tr(T.h3[:], T.y3[:], n3)
+    g.vector.wait_ge(s.xw, 32)
+    g.vector.wait_ge(s.aS0, 2 * ncp)
+    npl = cpy(b32(T.plq[:]), b32(T.xwq[:]).indirect(T.offl[:]), noffl)
+    wait("a", g.scalar, "sv", noffl)
+    g.scalar.wait_ge(s.xw, 32)
+    g.scalar.wait_ge(s.aS0, 2 * ncp)
+    nal = SA(lambda: g.scalar.activation(T.pls[:], T.xws[:].indirect(T.offl[:]), AF.Copy))
+
+    wait("g", g, "sv", npl)
+    send(cf_, b8(T.llq[:]), b8(T.plq[:]), "aL")
+    wait("g", g, "sa", nal)
+    send(cf_, T.lls[:], T.pls[:], "aL")
+
+    n3 = tt(T.a3[:], T.h3[:], T.m3[:], A.max, max(n3, nm3))
+    if fline:
+        ts(T.la[:], t, u, 0.0, A.add, A.max, d=nt)
+    else:
+        ts(T.la[:], t, -1.0, ba, A.mult, A.add, d=max(nt, nba))
+    nwa = ts(T.wa[:], t, 0.0, BIG if fline else -BIG, A.is_ge, A.mult)
+    cpy(T.o3[L, :], T.a3[L, lo], n3)
+    no3 = cpy(T.o3[U, :], T.a3[U, hi])
+    nwb = ts(T.wb[:], t, second, BIG, A.is_ge, A.mult)
+    lb, nlb = t, nwb
+    if fline:
+        lb, nlb = T.lb[:], ts(T.lb[:], t, -1.0, C1 - 1.0, A.mult, A.add)
+    g.vector.wait_ge(s.vps, 64)
+    vsa(nwf)
+    n = cpy(T.winf[:].indirect(T.o3[:]), T.valb[:], no3)
+    tt(T.ma[:], T.la[:], T.wa[:], A.max if fline else A.add, nwa)
+    nw = tr(T.tf[:], T.winf[:, 0:S_], n)
+    nm = tt(T.mb[:], lb, T.wb[:], A.max, nlb)
+    g.vector.wait_ge(s.sg, 6)
+    tt(T.yf[:, 0:24], T.tf[:, 0:S_:32], T.tf[:, 16:S_:32], A.min, nw)
+    nw = tt(T.yf[:, 32:56], T.tf[:, 0:S_:32], T.tf[:, 16:S_:32], A.min)
+    nm = tt(T.fm[:], T.ma[:], T.mb[:], A.min if fline else A.max, nm)
+    nw = tr(T.ytf[:], T.yf[:], nw)
+    nh = ts(T.fh[:], T.fm[:], T.hf[:], None, A.add, d=nm)
+    tr(T.yff[:, 0:32], T.ytf[:, 0:64:2], nw)
+    nw = tr(T.yff[:, 32:64], T.ytf[:, 1:64:2])
+    ts(na_, u, v, nl, A.add, A.add, d=nc3)
+    ts(T.sw[L, :], T.yff[U, :], 256.0, None, A.add, d=nw)
+    ts(T.sw[U, :], T.yff[L, :], -256.0, None, A.add)
+    n = tt(T.fl[:], T.yff[:], T.fh[:], A.min, nh)
+    nln = cpy(nq, fst) if even else tt(nq, nl, fst, A.subtract)
+    n = tt(T.fl2[:], T.fl[:], T.sw[:], A.min, n)
+    noff = ts(T.offf[:], T.fl2[:], T.ho[:], float(ZC), A.add, A.min, d=n)
+
+    def mm(bank, o, qb, sbuf, a, n):
+        g.tensor.matmul_mx(T.ps[:, 512 * bank:512 * bank + n], T.wq[:, 128 * o:128 * o + 128], T.ws[:, 128 * o:128 * o + 128],
+                           qb[:, a:a + n], sbuf[:, a:a + n], True, True).then_inc(s.st, 1)
+        cnt["st"] += 1
+    g.tensor.wait_ge(s.sv, nwq)
+    for bank, (qb, sbuf, a, n, sem, k) in enumerate(((T.xq, T.xs, 0, 512, None, 0), (T.xwq, T.xws, 0, 256, "aS0", 2 * ncp),
+                                                     (T.leq, T.les, 0, EARLY, "aE", 2 * nmf), (T.llq, T.lls, 0, 256, "aL", 2 * nmf))):
+        if sem:
+            g.tensor.wait_ge(s[sem], k)
+        for o in range(2):
+            mm(2 * bank + o, o, qb, sbuf, a, n)
+    res = (T.res0, T.res1)
+    base = (0, T_, FB, FB + EARLY)
+    width = (512, 256, EARLY, 256)
+    for b in range(3):
+        for o in range(2):
+            wait("a", g.scalar, "st", 2 * b + o + 1)
+            ncop = act(res[o][:, base[b]:base[b] + width[b]], T.ps[:, 512 * (2 * b + o):512 * (2 * b + o) + width[b]])
+    wait("a", g.scalar, "st", 8)
+    nlast = act(res[1][:, base[3]:base[3] + 256], T.ps[:, 512 * 7:512 * 7 + 256])
+    wait("v", g.vector, "st", 7)
+    n = cpy(res[0][:, base[3]:base[3] + 256], T.ps[:, 512 * 6:512 * 6 + 256])
+    g.vector.wait_ge(s.sg, 8)
+    g.scalar.wait_ge(s.sg, 8)
+    vsa(ncop)
+    for k in range(len(CUTS) - 1):
+        a, b = CUTS[k], CUTS[k + 1]
+        c = a // 16 + (8 if a >= S_ // 2 else 0)
+        of = T.offf[:, c:c + (b - a) // 16]
+        n0 = cpy(T.yt_0[:, a:b], T.res0[:].indirect(of), max(n, noff))
+        n1 = SA(lambda: g.scalar.activation(T.yt_1[:, a:b], T.res1[:].indirect(of), AF.Copy), noff, nlast)
+        if k == 0:
+            wait("s", g.sync, "sv", nln)
+            g.sync.dma_start(T.ln[:, :], T.lnt[0:1, :]).then_inc(s.yst, 16)
+        wait("s", g.sync, "sv", n0)
+        g.sync.dma_start(T.y[:, a:b], T.yt_0[:, a:b]).then_inc(s.yst, 16)
+        wait("s", g.sync, "sa", n1)
+        g.sync.dma_start(T.y[:, S_ + a:S_ + b], T.yt_1[:, a:b]).then_inc(s.yst, 16)
+    g.sync.wait_ge(s.yst, 16 * (2 * len(CUTS) - 1))
+    g.wait_ge(s.loc, cnt["loc"])

@@ -1,16 +1,12 @@
-import numpy as np
 from concourse.bass import DstId, RemoteDMATransfer
-from concourse.mybir import dt, AluOpType, AxisListType, ActivationFunctionType
+from concourse.mybir import dt, AluOpType, ActivationFunctionType
 
-T_, S_, C0, C1 = 512, 768, 256, 480
-EARLY = C1 - C0
-OWN = T_ - EARLY
-FB = T_ + C0
-RW = FB + C1 + 32
-ZC = FB + C1
-CUTS = (0, 128, 384, 768)
-FAR = 16 * 127 + 16
-LS = 256.0 + C0 - EARLY
+T_, S_, C = 512, 768, 256
+H = S_ // 2
+W0 = 2 * C
+D1, D2 = 1488, 800
+OWN, HOP, ZC = 2 * C, 2 * C + T_, 3 * C + T_
+VB = OWN + 256
 NONE = 4096.0
 BIG = 8192.0
 
@@ -23,38 +19,31 @@ def sb(n, d):
 
 
 SCRATCH = {
-    "dmt": sb(68, I32),
+    "dmt": sb(36, I32), "dm2": sb(64, I32),
     "xt": sb(2048, BF), "wt": sb(1024, BF),
-    "xq": sb(512, Q4), "xs": sb(512, U8), "wq": sb(256, Q4), "ws": sb(256, U8),
-    "xwq": sb(C0 + OWN, Q4), "xws": sb(C0 + OWN, U8),
-    "p0q": sb(256, Q4), "p0s": sb(256, U8),
-    "peq": sb(EARLY, Q4), "pes": sb(EARLY, U8), "plq": sb(256, Q4), "pls": sb(256, U8),
-    "leq": sb(EARLY, Q4), "les": sb(EARLY, U8), "llq": sb(256, Q4), "lls": sb(256, U8),
-    "one": sb(32, F32), "half": sb(32, F32), "hpm": sb(32, F32), "cb": sb(1, F32), "sgn": sb(1, F32),
-    "ho": sb(1, F32), "hf": sb(1, F32),
-    "pi": sb(2, I32), "pint": sb(8, I32), "pf": sb(8, F32),
-    "val0": sb(256, BF), "valb": sb(256, BF), "dd0": sb(32, F32), "dd": sb(32, F32), "i480": sb(64, F32), "i48": sb(64, F32),
-    "dfl": sb(16, F32),
-    "ta": sb(16, I32), "tb": sb(16, I32), "td": sb(32, I32),
-    "z0": sb(96, F32), "zt0": sb(64, F32), "car0": sb(1, F32), "pt0": sb(32, F32), "zb0": sb(32, F32), "m0": sb(32, F32),
-    "a0": sb(32, F32), "h0": sb(32, F32), "hm": sb(32, F32), "o0": sb(16, U16), "slt": sb(32, F32),
-    "z3": sb(96, F32), "zt3": sb(64, F32), "car3": sb(1, F32), "pt3": sb(32, F32), "zb3": sb(32, F32), "m3": sb(32, F32),
-    "x3": sb(32, F32), "w3": sb(32, F32), "y3": sb(32, F32), "a3": sb(32, F32), "h3": sb(32, F32), "o3": sb(16, U16),
-    "winu": sb(1024 + FAR, BF), "tu": sb(960, BF), "yu": sb(128, F32), "ytu": sb(128, F32), "yuu": sb(64, F32),
-    "off0": sb(16, U16), "offu": sb(14, U16),
-    "winf": sb(1024 + FAR, BF), "tf": sb(S_, BF), "yf": sb(64, F32), "ytf": sb(64, F32), "yff": sb(64, F32), "sw": sb(64, F32),
-    "slu": sb(32, BF), "slin": sb(32, BF),
-    "rexp": sb(32, F32), "ct": sb(32, F32), "cuv": sb(8, F32), "rexp3": sb(32, F32), "ct3": sb(32, F32),
-    "cf": sb(4, F32), "cg": sb(4, F32),
-    "lc": sb(16, F32), "offl": sb(16, U16),
-    "sc": sb(16, F32), "lnt": sb(2, F32),
-    "tl": sb(64, F32), "la": sb(64, F32), "wa": sb(64, F32), "lb": sb(64, F32), "wb": sb(64, F32),
-    "ma": sb(64, F32), "mb": sb(64, F32), "fm": sb(64, F32), "fh": sb(64, F32), "fl": sb(64, F32), "fl2": sb(64, F32),
-    "offf": sb(64, U16),
-    "res0": sb(RW, F32), "res1": sb(RW, F32), "yt_0": sb(768, F32), "yt_1": sb(768, F32),
+    "xq": sb(T_, Q4), "xs": sb(T_, U8), "wq": sb(256, Q4), "ws": sb(256, U8),
+    "xwq": sb(2 * C, Q4), "xws": sb(2 * C, U8),
+    "p0q": sb(C, Q4), "p0s": sb(C, U8), "peq": sb(C, Q4), "pes": sb(C, U8), "plq": sb(C, Q4), "pls": sb(C, U8),
+    "leq": sb(C, Q4), "les": sb(C, U8), "llq": sb(C, Q4), "lls": sb(C, U8),
+    "pi": sb(2, I32), "pint": sb(2, I32), "pf": sb(2, F32), "one": sb(64, F32), "oneb": sb(C, BF), "d0": sb(32, F32),
+    "eqv": sb(1, F32), "sgn": sb(1, F32), "dmp": sb(1, F32), "ini": sb(1, F32), "sad": sb(1, F32), "k2": sb(8, F32),
+    "val0": sb(256, BF), "valb": sb(256, BF), "valc": sb(128, BF), "i0": sb(64, F32), "ii": sb(56, F32), "im": sb(56, F32),
+    "ni": sb(56, F32),
+    "t1": sb(32, I32), "z1": sb(32, F32), "x1": sb(64, F32), "xt1": sb(64, F32), "pt1": sb(32, F32), "a1": sb(32, F32),
+    "o1": sb(16, U16), "hm": sb(32, F32), "slu": sb(32, BF), "slin": sb(32, BF), "rx1": sb(64, F32), "ct1": sb(64, F32),
+    "winu": sb(D1 + 240, BF), "tu": sb(512, BF), "yu": sb(96, BF), "ytu": sb(64, BF), "yuu": sb(32, BF), "am": sb(16, BF),
+    "off0": sb(16, U16), "offe": sb(16, U16), "offl": sb(16, U16),
+    "cf": sb(4, F32), "cg": sb(4, F32), "sc": sb(8, F32),
+    "t2": sb(64, I32), "z2": sb(66, BF), "x2": sb(128, BF), "xt2": sb(128, BF), "pt2": sb(64, F32), "w2": sb(48, F32),
+    "y2": sb(48, F32), "a2": sb(48, F32), "o2": sb(8, U16), "rx2": sb(32, F32), "ct2": sb(40, F32),
+    "winf": sb(D2 + 240, BF), "tf": sb(S_, BF), "ya": sb(24, F32), "yb": sb(24, F32), "yc": sb(24, F32), "yf": sb(64, F32),
+    "ytf": sb(64, F32), "yff": sb(64, F32),
+    "la": sb(56, F32), "lb": sb(56, F32), "wa": sb(56, F32), "wb": sb(56, F32), "ma": sb(56, F32), "mb": sb(56, F32),
+    "fm": sb(56, F32), "fl": sb(56, F32), "offf": sb(56, U16),
+    "res0": sb(ZC + 8, F32), "res1": sb(ZC + 8, F32), "yt_0": sb(S_, F32), "yt_1": sb(S_, F32),
     "ps": ("psum", [128, 4096], F32),
 }
-SEMAPHORES = ["sv", "sa", "st", "sg", "dml", "xl0", "xl1", "wl", "xw", "vps", "yst",
+SEMAPHORES = ["sv", "sa", "st", "sg", "dml", "dm2", "xl0", "xl1", "wl", "vps", "yst",
               "aDM", "aS0", "aSL", "aCNT", "aE", "aL", "loc"]
 
 
@@ -64,14 +53,16 @@ def rank_program(g, core, T, topo):
         return
     A = AluOpType
     AF = ActivationFunctionType
-    X = AxisListType.X
     rp, rf, rg = q ^ 1, q ^ 2, q ^ 3
     cp, cf_, cg_ = T.cores[rp], T.cores[rf], T.cores[rg]
     P, Fb, G, Qb = 1 << rp, 1 << rf, 1 << rg, 1 << q
     s = T.sem
-    cnt = {"sv": 0, "sa": 0, "st": 0, "loc": 0}
+    cnt = {"sv": 0, "sa": 0, "st": 0, "sg": 0, "loc": 0}
     seen = {}
     L, U = slice(0, 64), slice(64, 128)
+    QS = Q0, Q1, Q2, Q3 = tuple(slice(32 * k, 32 * k + 32) for k in range(4))
+    G0 = slice(0, 16)
+    even, local_first, fline = q < rp, q < rf, rf < rg
 
     def wait(name, eng, sem, n):
         if n > 0 and seen.get((name, sem), 0) < n:
@@ -93,13 +84,16 @@ def rank_program(g, core, T, topo):
         r.then_inc(s.sa, 1)
         return cnt["sa"]
 
-    def vsa(n):
-        wait("v", g.vector, "sa", n)
+    def vw(sem, n):
+        wait("v", g.vector, sem, n)
 
     def ts(out, in0, s1, s2, op0, op1=None, d=0):
         if op1 is None:
             return V(lambda: g.vector.tensor_scalar(out, in0, s1, s2, op0), d)
         return V(lambda: g.vector.tensor_scalar(out, in0, s1, s2, op0, op1), d)
+
+    def line(out, in0, a, b, d=0):
+        return ts(out, in0, a, b, A.mult, A.add, d)
 
     def tt(out, a, b, op, d=0):
         return V(lambda: g.vector.tensor_tensor(out, a, b, op), d)
@@ -110,22 +104,23 @@ def rank_program(g, core, T, topo):
     def tr(out, in_, d=0):
         return V(lambda: g.vector.transpose(out, in_), d)
 
-    def red(out, in_, d=0):
-        return V(lambda: g.vector.tensor_reduce(out, in_, X, A.add), d)
-
-    def scan(out, d1, init, d=0):
-        return V(lambda: g.vector.tensor_tensor_scan(out, T.one[:], d1, init, A.mult, A.add), d)
+    def scan(out, d0, d1, init, d=0):
+        return V(lambda: g.vector.tensor_tensor_scan(out, d0, d1, init, A.mult, A.add), d)
 
     def fill(ap, c, d=0):
         return V(lambda: g.vector.memset(ap, c), d)
 
-    def act(out, in_, v=0, a=0, f=AF.Copy, scale=None, bias=None):
-        kw = {}
-        if scale is not None:
-            kw["scale"] = scale
-        if bias is not None:
-            kw["bias"] = bias
-        return SA(lambda: g.scalar.activation(out, in_, f, **kw), v, a)
+    def quant(qb, sbuf, src, a):
+        return V(lambda: g.vector.quantize_mx(qb[:, a:a + 128], sbuf[:, a:a + 128], src[:, 4 * a:4 * a + 512]))
+
+    def spread(off, src, d=0):
+        return [ts(off[part, :], src, 256.0, None, A.add, d=d) for part in QS][-1]
+
+    def iota(out, pattern, base, cm=0, whole=False):
+        kw = {} if whole else {"allow_small_or_imprecise_dtypes": True}
+        g.iota(out, pattern, base, cm, **kw).then_inc(s.sg, 1)
+        cnt["sg"] += 1
+        return cnt["sg"]
 
     def send(dst, out, in_, rsem):
         rid, pid, _se = topo.addr(dst)
@@ -141,263 +136,294 @@ def rank_program(g, core, T, topo):
     def b32(ap):
         return ap.bitcast(dt.uint32)
 
-    even = q < rp
-    ob = 4 if even else 36
-    for k in range(8):
-        e = g.sync if k % 2 == 0 else g.scalar
-        o = ob - k % 2
-        e.dma_start(T.dmt[16 * k:16 * k + 16, o:o + 32], T.dm[:, :]).then_inc(s.dml, 16)
-    g.sync.dma_start(T.xt[:, 4 * EARLY:2048], T.x[:, 4 * EARLY:2048]).then_inc(s.xl0, 16)
-    g.scalar.dma_start(T.xt[:, 0:4 * EARLY], T.x[:, 0:4 * EARLY]).then_inc(s.xl1, 16)
-    g.scalar.dma_start(T.wt[:], T.w[:]).then_inc(s.wl, 16)
+    def pick(oq, os_, wq_, ws_, off, v):
+        nq_ = cpy(b32(oq), b32(wq_).indirect(off), v)
+        return nq_, SA(lambda: g.scalar.activation(os_, ws_.indirect(off), AF.Copy), v)
 
-    FL = {"allow_small_or_imprecise_dtypes": True}
-    g.iota(T.pi[:, 0:1], [[1, 1]], 0, 1).then_inc(s.sg, 1)
-    g.iota(T.val0[:], [[32, 16], [1, 16]], -256, 0, **FL).then_inc(s.sg, 1)
-    g.iota(T.dd0[:], [[0, 2], [16, 16]], 1024, 0, **FL).then_inc(s.sg, 1)
-    g.iota(T.i480[:], [[S_ // 2, 2], [16, 32]], 0, 0, **FL).then_inc(s.sg, 1)
-    g.wait_ge(s.dml, 128)
-    send(cp, T.dmt[:, ob:ob + 31], T.dmt[:, ob:ob + 31], "aDM")
-    g.iota(T.yu[:], [[0, 128]], 0, 0, **FL).then_inc(s.sg, 1)
+    def send_pick(dst, lq, ls, pq, ps_, n, rsem):
+        wait("g", g, "sv", n[0])
+        send(dst, b8(lq), b8(pq), rsem)
+        wait("g", g, "sa", n[1])
+        send(dst, ls, ps_, rsem)
 
-    nwu = fill(T.winu[:, 0:512], -NONE)
-    g.vector.wait_ge(s.sg, 1)
+    ob = 0 if even else 32
+    ndm2 = fill(T.dm2[:, ob:ob + 32], 0)
+    fill(T.dmt[G0, 0:4], 0)
+    fill(T.winu[:, W0:2 * W0], -NONE)
+    nwu = fill(T.oneb[U, :], 1.0)
+    gpi = iota(T.pi[:, 0:1], [[1, 1]], 0, 1, whole=True)
+    vw("sg", gpi)
     ts(T.pint[:, 0:1], T.pi[:, 0:1], 16, None, A.bitwise_and)
     n = ts(T.pint[:, 1:2], T.pi[:, 0:1], 15, None, A.bitwise_and)
     fill(T.one[:], 1.0)
-    fill(T.z0[L, 31:32], C0 / 16.0)
-    npf = cpy(T.pf[:, 0:2], T.pint[:, 0:2], n)
-    fill(T.z0[U, 31:32], -2.0 / 32)
-    fill(T.z0[U, 48:64], 0.0)
-    fill(T.sgn[L, :], -2.0)
-    nsgn = fill(T.sgn[U, :], 2.0)
-    g.vector.wait_ge(s.sg, 2)
-    ts(T.valb[:], T.val0[:], T.pf[:, 0:1], None, A.add, d=npf)
+    for part, c in ((Q0, G), (Q1, P), (U, Fb)):
+        fill(T.eqv[part, :], float(c))
+    ts(T.pf[:, 0:1], T.pint[:, 0:1], 16.0, None, A.mult, d=n)
+    npf = cpy(T.pf[:, 1:2], T.pint[:, 1:2])
+    h16, s16 = T.pf[:, 0:1], T.pf[:, 1:2]
+    scan(T.winu[U, W0:2 * W0:2], T.oneb[U, :], T.oneb[U, :], -257.0)
+    for part, c in ((Q0, -2.0), (Q1, 2.0), (U, 2.0)):
+        fill(T.sgn[part, :], c)
+    line(T.dmp[:], s16, 16.0, float(D1), npf)
+    ts(T.d0[:], T.one[:, 0:32], h16, None, A.is_gt)
+    for part, c in ((Q0, 2 * W0), (Q1, W0 - 2), (Q2, W0 - 2), (Q3, -2)):
+        nk = line(T.ini[part, :], T.pf[part, 1:2], -1.0, c + 16.0)
 
-    act(T.winu[:, 512:960], T.winu[:, 0:448], nwu)
-    nwf0 = act(T.winf[:, 0:512], T.winu[:, 0:512], scale=-1.0)
+    g.sync.dma_start(T.dmt[0:16, 4:36], T.dm[:, :]).then_inc(s.dml, 16)
+    g.scalar.dma_start(T.dmt[16:32, 3:35], T.dm[:, :]).then_inc(s.dml, 16)
+    for name, e, r in (("s", g.sync, 0), ("a", g.scalar, 16)):
+        wait(name, e, "sv", ndm2)
+        e.dma_start(T.dm2[r:r + 16, ob:ob + 32], T.dm[:, :]).then_inc(s.dm2, 16)
+    g.scalar.dma_start(T.xt[:, 0:1024], T.x[:, 0:1024]).then_inc(s.xl0, 16)
+    g.sync.dma_start(T.xt[:, 1024:2048], T.x[:, 1024:2048]).then_inc(s.xl1, 16)
+    g.scalar.dma_start(T.wt[:], T.w[:]).then_inc(s.wl, 16)
 
-    g.vector.wait_ge(s.dml, 128)
-    ts(T.ta[L, :], T.dmt[L, ob:ob + 31:2], G, None, A.bitwise_and)
-    na = ts(T.ta[U, :], T.dmt[U, ob:ob + 31:2], Fb, None, A.bitwise_and)
-    nb = ts(T.tb[L, :], T.dmt[L, ob:ob + 31:2], P | G, None, A.bitwise_and)
-    fill(T.hpm[L, :], -0.5)
-    ts(T.z0[:, 32:48], T.ta[:], 0.0, T.sgn[:], A.is_gt, A.mult, d=max(na, nsgn))
-    nz = ts(T.z0[L, 48:64], T.tb[L, :], float(P), -2.0, A.is_equal, A.mult, d=nb)
-    fill(T.hpm[U, :], 0.5)
-    fill(T.cb[L, :], float(C0))
-    n = scan(T.z0[:, 64:96], T.z0[:, 31:63], 0.0, nz)
-    nzb = ts(T.zb0[:], T.z0[:, 32:64], 0.0, 65536.0, A.not_equal, A.mult)
-    g.vector.wait_ge(s.sg, 3)
-    ndd = ts(T.dd[:], T.dd0[:], T.pf[:, 1:2], None, A.add)
-    n = tr(T.zt0[:], T.z0[:, 32:96], n)
-    fill(T.cb[U, :], 1.0)
-    fill(T.hm[:], 0.0)
-    n = red(T.car0[:], T.zt0[:, 32:64], n)
-    nm = tt(T.m0[:], T.dd[:], T.zb0[:], A.subtract, max(nzb, ndd))
-    fill(T.half[:], 0.5)
-    np0 = scan(T.pt0[:], T.zt0[:, 0:32], T.car0[:], n)
-    fill(T.z3[:, 31:32], -2.0 / 32)
-    fill(T.ho[L, :], 256.0)
-    n = tr(T.h0[:], T.pt0[:], np0)
-    nrx = ts(T.rexp[:], T.hpm[:], T.pt0[:, 31:32], T.cb[:], A.mult, A.add)
-    fill(T.ho[U, :], 512.0)
-    n = tt(T.a0[:], T.h0[:], T.m0[:], A.max, max(n, nm))
-    nct = tr(T.ct[:], T.rexp[:], nrx)
-    fill(T.hf[L, :], FB - 256.0)
-    n = tt(T.hm[:, 0:16], T.a0[:, 0:16], T.a0[:, 16:32], A.min, n)
-    fill(T.hf[U, :], FB - 512.0)
-    g.vector.wait_ge(s.sg, 4)
-    ni48 = ts(T.i48[:], T.i480[:], T.pf[:, 1:2], None, A.add)
-    n = cpy(T.o0[:], T.hm[:, 0:16], n)
-    nslt = tr(T.slt[:], T.hm[:])
-    vsa(nwf0)
-    nwin = cpy(T.winu[:].indirect(T.o0[:]), T.valb[:], n)
-    act(T.cuv[L, 0:4], T.ct[L, 15:19], nct)
-    nslu = act(T.slu[:], T.slt[:], nslt, scale=0.5)
-    act(T.cuv[U, 0:4], T.ct[L, 15:19])
-    act(T.cuv[L, 4:8], T.ct[U, 15:19])
-    ncuv = act(T.cuv[U, 4:8], T.ct[U, 15:19])
-    nwf = act(T.winf[:, 512:S_], T.winf[:, 0:S_ - 512], 0, nwf0)
+    gval = iota(T.val0[:], [[1, 16], [16, 16]], -256)
+    gi0 = iota(T.i0[Q0, :], [[H, 2], [16, 32]], 0)
+    g.wait_ge(s.dm2, 32)
+    send(cp, T.dm2[:, ob:ob + 32], T.dm2[:, ob:ob + 32], "aDM")
+    gyu = iota(T.yu[:], [[0, 96]], 0)
+    gyf = iota(T.yf[Q0, :], [[0, 64]], 0)
+    for b in (T.res0, T.res1):
+        gz = iota(b[:, ZC:ZC + 8], [[0, 8]], 0)
+
+    s0 = T.pf[Q0, 1:2]
+    kini, kthr, kdmp, ksl = (T.k2[Q0, j:j + 1] for j in range(4))
+    I, IM, NI = T.ii[Q0, :], T.im[Q0, :], T.ni[Q0, :]
+    sh = VB if local_first and fline else 0
+    g.vector.wait_ge(s.dml, 32)
+    for part, m in ((Q0, G), (Q1, P | G), (Q2, Fb), (Q3, Fb)):
+        n = ts(T.t1[part, :], T.dmt[Q0, 3:35], m, None, A.bitwise_and)
+    ts(T.sad[:], s16, -16.0, None, A.add)
+    line(kini, s0, -1.0, 14.0 if local_first else 16.0 + W0)
+    line(kthr, s0, -1.0, S_ + 16.0)
+    line(kdmp, s0, 16.0, float(D2))
+    n = ts(T.z1[:], T.t1[:], T.eqv[:], T.sgn[:], A.is_equal, A.mult, d=n)
+    ts(T.x1[:, 32:64], T.t1[:], T.eqv[:], T.dmp[:], A.not_equal, A.mult)
+    vw("sg", gval)
+    nval = ts(T.valb[:], T.val0[:], h16, None, A.add)
+    n = scan(T.x1[:, 0:32], T.d0[:], T.z1[:], 0.0, n)
+    line(ksl, s0, 0.5, -(W0 + 16) / 2)
+    fill(T.z2[G0, 0:1], 0.0)
+    vw("sg", gi0)
+    nii = ts(I, T.i0[Q0, 0:56], s0, None, A.add)
+    n = tr(T.xt1[:], T.x1[:], n)
+    cpy(T.valc[L, :], T.valb[L, 0:128], nval)
+    nvc = cpy(T.valc[U, :], T.valb[U, 128:256])
+    npt = scan(T.pt1[:], T.one[:, 0:32], T.xt1[:, 0:32], T.ini[:], n)
     g.vector.wait_ge(s.xl0, 16)
-    nxq0 = V(lambda: g.vector.quantize_mx(T.xq[:, EARLY:T_], T.xs[:, EARLY:T_], T.xt[:, 4 * EARLY:2048]))
-    n = tr(T.tu[:, 0:512], T.winu[:, 0:512], nwin)
-    ndfl = ts(T.dfl[:], T.i48[:, 0:16], -LS, None, A.add, d=ni48)
-    g.vector.wait_ge(s.aDM, ncp)
-    n3 = ts(T.td[:], T.dmt[:, 4:67:2], Qb, None, A.bitwise_and)
-    g.vector.wait_ge(s.sg, 5)
-    tt(T.yu[:, 0:16], T.tu[:, 0:512:32], T.tu[:, 16:512:32], A.max, n)
-    n = tt(T.yu[:, 32:48], T.tu[:, 0:512:32], T.tu[:, 16:512:32], A.max)
-    n3 = ts(T.z3[:, 32:64], T.td[:], 0.0, 2.0, A.is_gt, A.mult, d=n3)
-    n = tr(T.ytu[:, 0:64], T.yu[:, 0:64], n)
-    n3 = scan(T.z3[:, 64:96], T.z3[:, 31:63], 0.0, n3)
-    ny = tr(T.yuu[:, 0:32], T.ytu[:, 0:64:2], n)
-    g.vector.wait_ge(s.xl1, 16)
-    V(lambda: g.vector.quantize_mx(T.xq[:, 0:EARLY], T.xs[:, 0:EARLY], T.xt[:, 0:4 * EARLY]))
-    ts(T.off0[L, :], T.yuu[L, 0:16], 256.0, None, A.add, d=ny)
-    noff0 = ts(T.off0[U, :], T.yuu[L, 0:16], 256.0, None, A.add)
-    ts(T.offu[L, :], T.yuu[U, 0:14], 256.0, None, A.add)
-    n3 = tr(T.zt3[:], T.z3[:, 32:96], n3)
-    nq0 = cpy(b32(T.p0q[:]), b32(T.xq[:]).indirect(T.off0[:]), noff0)
-    na0 = SA(lambda: g.scalar.activation(T.p0s[:], T.xs[:].indirect(T.off0[:]), AF.Copy), noff0)
-    noffu = ts(T.offu[U, :], T.yuu[U, 0:14], 256.0, None, A.add)
-    n3 = red(T.car3[:], T.zt3[:, 32:64], n3)
-    nzb = ts(T.zb3[:], T.z3[:, 32:64], 0.0, 65536.0, A.not_equal, A.mult)
-    npe = cpy(b32(T.peq[:]), b32(T.xq[:]).indirect(T.offu[:]), noffu)
-    nae = SA(lambda: g.scalar.activation(T.pes[:], T.xs[:].indirect(T.offu[:]), AF.Copy), noffu)
+    quant(T.xq, T.xs, T.xt, 0)
+    na1 = tt(T.a1[:, 16:32], T.pt1[:, 16:32], T.xt1[:, 48:64], A.max, npt)
+    for o_, c, i_ in ((L, 0, L), (U, 0, L), (L, 32, U), (U, 32, U)):
+        nrx = ts(T.rx1[o_, c:c + 32], T.one[i_, 0:32], T.pt1[i_, 31:32], None, A.mult)
+    line(NI, I, -1.0, 2 * C - 1.0 - VB + sh, nii)
+    n = ts(T.o1[:], T.a1[:, 16:32], T.sad[:], None, A.add, d=na1)
+    nct = tr(T.ct1[:], T.rx1[:], nrx)
+    for c, part in ((0, Q0), (16, Q1)):
+        nhm = ts(T.hm[Q0, c:c + 16], T.a1[part, 16:32], 0.5, None, A.mult)
+    nwin = cpy(T.winu[:].indirect(T.o1[:]), T.valb[:], n)
 
-    wait("s", g.sync, "sv", nxq0)
-    g.sync.dma_start(b8(T.xwq[:, C0:C0 + OWN]), b8(T.xq[:, EARLY:T_])).then_inc(s.xw, 16)
-    g.sync.dma_start(T.xws[:, C0:C0 + OWN], T.xs[:, EARLY:T_]).then_inc(s.xw, 16)
-    g.sync.wait_ge(s.aSL, ncp)
-    for k in range(4, 8):
-        h = k % 2
-        g.sync.dma_start(T.valb[16 * k:16 * k + 1, :], T.slin[0:16, 16 * h:16 * h + 16]).then_inc(s.vps, 16)
-
-    wait("g", g, "sa", nslu)
-    send(cp, T.slin[:], T.slu[:], "aSL")
-    wait("g", g, "sa", ncuv)
+    g.scalar.wait_ge(s.xl0, 16)
+    nwf = SA(lambda: g.scalar.activation(T.winf[:, 0:S_], T.xt[:, 0:S_], AF.Identity, scale=0.0, bias=-NONE))
+    wait("g", g, "sv", nct)
     trs = []
-    for dst, land, c, h in ((cf_, T.cf, 4, 0), (cg_, T.cg, 0, 1)):
+    for dst, land, h in ((cg_, T.cg, 0), (cf_, T.cf, 1)):
         en = topo.engines(core, dst)
         en = en[:len(en) // 2] if h == 0 else en[len(en) // 2:]
         rid, pid, _se = topo.addr(dst)
         trs.append(RemoteDMATransfer(dst_ids=[DstId(rid=rid, pnc=pid)], dma_engine_mask=sum(1 << e for e in en),
-                                     remote_sem=s.aCNT, src=T.cuv[:, c:c + 4], dst=land[:]))
+                                     remote_sem=s.aCNT, src=T.ct1[:, 32 * h + 28:32 * h + 32], dst=land[:]))
         cnt["loc"] += len(en)
     g.remote_dma_fused(trs, local_sem=s.loc)
-    for b, a, n in ((T.yf, 0, 64), (T.res0, ZC, 32), (T.res1, ZC, 32)):
-        g.iota(b[:, a:a + n], [[0, n]], 0, 0, **FL).then_inc(s.sg, 1)
-    wait("g", g, "sv", nq0)
-    send(cp, b8(T.xwq[:, 0:C0]), b8(T.p0q[:]), "aS0")
-    wait("g", g, "sa", na0)
-    send(cp, T.xws[:, 0:C0], T.p0s[:], "aS0")
-    wait("g", g, "sv", npe)
-    send(cf_, b8(T.leq[:]), b8(T.peq[:]), "aE")
-    wait("g", g, "sa", nae)
-    send(cf_, T.les[:], T.pes[:], "aE")
 
-    local_first = q < rf
-    u, v = T.cf[:, 0:1], T.cg[:, 0:1]
-    nf2, ba = T.sc[:, 0:1], T.sc[:, 1:2]
-    fline = rf < rg
-    nl, fst = T.ct3[:, 31:32], T.ct3[:, 15:16]
-    na_, nq = T.lnt[:, 0:1], T.lnt[:, 1:2]
-    lo, hi = (slice(0, 16), slice(16, 32)) if even else (slice(16, 32), slice(0, 16))
-    first, second = (u, v) if fline else (v, u)
-    t = T.tl[:]
-    x3 = T.pt3 if local_first else T.x3
-    nu = tr(T.tu[:, 512:960], T.winu[:, 512:960], nwin)
-    npt = np3 = scan(T.pt3[:], T.zt3[:, 0:32], T.car3[:], n3)
-    nm3 = tt(T.m3[:], T.dd[:], T.zb3[:], A.subtract, nzb)
-    tt(T.yu[:, 64:80], T.tu[:, 448:960:32], T.tu[:, 464:960:32], A.max, nu)
-    nu = tt(T.yu[:, 96:112], T.tu[:, 448:960:32], T.tu[:, 464:960:32], A.max)
-    nrx3 = ts(T.rexp3[:], T.half[:], T.pt3[:, 31:32], 1.0, A.mult, A.add, d=npt)
-    g.vector.wait_ge(s.aCNT, nmf)
-    if not local_first:
-        n = ts(nf2, u, v, 2.0, A.add, A.mult)
-    nba = 0 if fline else ts(ba, v, -1.0, C1 - 1.0, A.mult, A.add)
-    nu = tr(T.ytu[:, 64:128], T.yu[:, 64:128], nu)
-    if not local_first:
-        np3 = ts(T.x3[:], T.pt3[:], nf2, None, A.add, d=n)
-    g.vector.wait_ge(s.wl, 16)
-    nwq = V(lambda: g.vector.quantize_mx(T.wq[:], T.ws[:], T.wt[:]))
-    nu = tr(T.yuu[:, 32:64], T.ytu[:, 64:128:2], nu)
-    n3 = ts(T.w3[:], x3[:], float(S_), 1.0 - S_, A.is_ge, A.mult, d=np3)
-    nc3 = tr(T.ct3[:], T.rexp3[:], nrx3)
-    nc = tt(T.lc[U, :], T.dfl[U, :], T.yuu[U, 32:48], A.max, max(nu, ndfl))
-    n3 = tt(T.y3[:], x3[:], T.w3[:], A.add, n3)
+    nhm = tt(T.hm[Q0, 16:32], T.hm[Q0, 0:16], T.hm[Q0, 16:32], A.min, nhm)
+    quant(T.xq, T.xs, T.xt, 128)
+    n = tr(T.tu[:], T.winu[:, W0:2 * W0], nwin)
+    vw("sg", gyu)
+    nhm = ts(T.yu[Q0, 80:96], T.hm[Q0, 16:32], ksl, None, A.add, d=nhm)
+    g.vector.wait_ge(s.aDM, ncp)
+    g.vector.wait_ge(s.dm2, 32)
+    n2 = ts(T.t2[Q0, :], T.dm2[Q0, :], Qb, None, A.bitwise_and)
+    ts(IM, I, -float(VB), None, A.add)
+    tt(T.yu[:, 0:16], T.tu[:, 0:512:32], T.tu[:, 16:512:32], A.max, n)
+    n = tt(T.yu[:, 32:48], T.tu[:, 0:512:32], T.tu[:, 16:512:32], A.max)
+    nslu = tr(T.slu[:], T.yu[:, 64:96], nhm)
+    g.vector.wait_ge(s.xl1, 16)
+    quant(T.xq, T.xs, T.xt, 256)
+    n = tr(T.ytu[:], T.yu[:, 0:64], n)
+    ts(T.z2[G0, 1:65], T.t2[G0, :], 0.0, 2.0, A.is_gt, A.mult, d=n2)
+    ts(T.x2[Q0, 64:128], T.t2[Q0, :], 0.0, kdmp, A.is_equal, A.mult)
+    n2 = ts(T.x2[Q0, 0:64], T.t2[Q0, :], 0.0, 2.0, A.is_gt, A.mult)
+    ny = tr(T.yuu[:], T.ytu[:, 0:64:2], n)
+    quant(T.xq, T.xs, T.xt, 384)
+    n2 = scan(T.x2[G0, 0:64], T.one[G0, :], T.z2[G0, 0:64], 0.0, n2)
+    n = tt(T.am[Q0, :], T.yuu[Q0, 0:16], T.yuu[Q1, 0:16], A.max, ny)
+    n0 = spread(T.off0, T.am[Q0, :], n)
+    n2 = tr(T.xt2[Q0, :], T.x2[Q0, :], n2)
+    u, v, ini2, nv = (T.sc[Q0, j:j + 1] for j in range(4))
     if local_first:
-        nt = ts(t, T.i48[:], nl, first, A.subtract, A.subtract, d=nc3)
+        ini2 = kini
     else:
-        nt = ts(t, T.i48[:], first, None, A.subtract)
-    ts(T.offl[L, :], T.lc[U, :], LS, None, A.add, d=nc)
-    noffl = ts(T.offl[U, :], T.lc[U, :], LS, None, A.add)
-    n3 = tr(T.h3[:], T.y3[:], n3)
-    g.vector.wait_ge(s.xw, 32)
+        g.vector.wait_ge(s.aCNT, nmf)
+        n2 = ts(ini2, kini, T.cf[Q0, 3:4], T.cg[Q0, 3:4], A.add, A.subtract)
+    ne = spread(T.offe, T.yuu[Q2, 0:16])
+    p0 = pick(T.p0q[:], T.p0s[:], T.xq[:], T.xs[:], T.off0[:], n0)
+    scan(T.pt2[Q0, 0:32], T.one[Q0, 0:32], T.xt2[Q0, 0:32], ini2, n2)
+    n2 = scan(T.pt2[Q0, 32:64], T.one[Q0, 0:32], T.xt2[Q0, 32:64], ini2)
+    pe = pick(T.peq[:], T.pes[:], T.xq[:], T.xs[:], T.offe[:], ne)
+
+    wait("g", g, "sv", nslu)
+    send(cp, T.slin[:], T.slu[:], "aSL")
+    send_pick(cp, T.xwq[:, 0:C], T.xws[:, 0:C], T.p0q[:], T.p0s[:], p0, "aS0")
+    send_pick(cf_, T.leq[:], T.les[:], T.peq[:], T.pes[:], pe, "aE")
+    g.sync.wait_ge(s.aSL, ncp)
+    wait("s", g.sync, "sv", nvc)
+    for k in range(4):
+        a, r, h = 32 + 64 * (k // 2) + 16 * (k % 2), 16 + 8 * (k // 2), 16 * (k % 2)
+        g.sync.dma_start(T.valc[a:a + 1, :], T.slin[r:r + 8, h:h + 16]).then_inc(s.vps, 16)
+
+    nw = ts(T.w2[Q0, :], T.pt2[Q0, 16:64], kthr, 1.0 - S_, A.is_ge, A.mult, d=n2)
+    nrx = ts(T.rx2[Q0, :], T.one[Q0, 0:32], T.pt2[Q0, 63:64], 0.5, A.add, A.mult)
+    g.vector.wait_ge(s.wl, 16)
+    quant(T.wq, T.ws, T.wt, 0)
+    n = tt(T.y2[Q0, :], T.pt2[Q0, 16:64], T.w2[Q0, :], A.add, nw)
+    nc2 = tr(T.ct2[Q0, 0:32], T.rx2[Q0, :], nrx)
+    nwq = quant(T.wq, T.ws, T.wt, 128)
+    n = tt(T.a2[Q0, :], T.y2[Q0, :], T.xt2[Q0, 80:128], A.max, n)
+    quant(T.xwq, T.xws, T.xt, C)
+    spread(T.offl, T.yuu[Q3, 0:16])
+    nxw = quant(T.xwq, T.xws, T.xt, C + 128)
+    oc, pc = (0, 32) if even else (32, 0)
+    for part, c in ((Q0, oc), (Q1, pc), (Q2, oc + 8), (Q3, pc + 8)):
+        no2 = ts(T.o2[part, :], T.a2[Q0, c:c + 8], T.sad[Q0, :], None, A.add, d=n)
+    if local_first:
+        g.vector.wait_ge(s.aCNT, nmf)
+    line(u, T.cf[Q0, 3:4], 0.5, -(W0 - 1) / 2 - sh)
+    nc2 = line(v, T.cg[Q0, 3:4], -0.5, (2 * W0 + 1) / 2 + sh)
+
     g.vector.wait_ge(s.aS0, 2 * ncp)
-    npl = cpy(b32(T.plq[:]), b32(T.xwq[:]).indirect(T.offl[:]), noffl)
-    wait("a", g.scalar, "sv", noffl)
-    g.scalar.wait_ge(s.xw, 32)
     g.scalar.wait_ge(s.aS0, 2 * ncp)
-    nal = SA(lambda: g.scalar.activation(T.pls[:], T.xws[:].indirect(T.offl[:]), AF.Copy))
-
-    wait("g", g, "sv", npl)
-    send(cf_, b8(T.llq[:]), b8(T.plq[:]), "aL")
-    wait("g", g, "sa", nal)
-    send(cf_, T.lls[:], T.pls[:], "aL")
-
-    n3 = tt(T.a3[:], T.h3[:], T.m3[:], A.max, max(n3, nm3))
-    if fline:
-        ts(T.la[:], t, u, 0.0, A.add, A.max, d=nt)
-    else:
-        ts(T.la[:], t, -1.0, ba, A.mult, A.add, d=max(nt, nba))
-    nwa = ts(T.wa[:], t, 0.0, BIG if fline else -BIG, A.is_ge, A.mult)
-    cpy(T.o3[L, :], T.a3[L, lo], n3)
-    no3 = cpy(T.o3[U, :], T.a3[U, hi])
-    nwb = ts(T.wb[:], t, second, BIG, A.is_ge, A.mult)
-    lb, nlb = t, nwb
-    if fline:
-        lb, nlb = T.lb[:], ts(T.lb[:], t, -1.0, C1 - 1.0, A.mult, A.add)
+    pl = pick(T.plq[:], T.pls[:], T.xwq[:], T.xws[:], T.offl[:], nxw)
+    send_pick(cf_, T.llq[:], T.lls[:], T.plq[:], T.pls[:], pl, "aL")
     g.vector.wait_ge(s.vps, 64)
-    vsa(nwf)
-    n = cpy(T.winf[:].indirect(T.o3[:]), T.valb[:], no3)
-    tt(T.ma[:], T.la[:], T.wa[:], A.max if fline else A.add, nwa)
-    nw = tr(T.tf[:], T.winf[:, 0:S_], n)
-    nm = tt(T.mb[:], lb, T.wb[:], A.max, nlb)
-    g.vector.wait_ge(s.sg, 6)
-    tt(T.yf[:, 0:24], T.tf[:, 0:S_:32], T.tf[:, 16:S_:32], A.min, nw)
-    nw = tt(T.yf[:, 32:56], T.tf[:, 0:S_:32], T.tf[:, 16:S_:32], A.min)
-    nm = tt(T.fm[:], T.ma[:], T.mb[:], A.min if fline else A.max, nm)
-    nw = tr(T.ytf[:], T.yf[:], nw)
-    nh = ts(T.fh[:], T.fm[:], T.hf[:], None, A.add, d=nm)
-    tr(T.yff[:, 0:32], T.ytf[:, 0:64:2], nw)
-    nw = tr(T.yff[:, 32:64], T.ytf[:, 1:64:2])
-    ts(na_, u, v, nl, A.add, A.add, d=nc3)
-    ts(T.sw[L, :], T.yff[U, :], 256.0, None, A.add, d=nw)
-    ts(T.sw[U, :], T.yff[L, :], -256.0, None, A.add)
-    n = tt(T.fl[:], T.yff[:], T.fh[:], A.min, nh)
-    nln = cpy(nq, fst) if even else tt(nq, nl, fst, A.subtract)
-    n = tt(T.fl2[:], T.fl[:], T.sw[:], A.min, n)
-    noff = ts(T.offf[:], T.fl2[:], T.ho[:], float(ZC), A.add, A.min, d=n)
+    vw("sa", nwf)
+    nsc = cpy(T.winf[:].indirect(T.o2[:]), T.valc[:], no2)
+
+    tot = T.ct2[Q0, 31:32]
+    if local_first:
+        na_, nq, lnv = T.ct2[Q0, 32:33], T.ct2[Q0, 33:34], T.ct2[31:32, 32:34]
+    else:
+        na_, nq, lnv = tot, T.ct2[Q0, 32:33], T.ct2[31:32, 31:33]
+    la, lb, wa, wb, ma, mb, fm = (t[Q0, :] for t in (T.la, T.lb, T.wa, T.wb, T.ma, T.mb, T.fm))
+    top = 2 * C - 1.0 - VB
+
+    def lines():
+        if local_first and fline:
+            ts(la, I, tot, -float(VB), A.subtract, A.add)
+            ts(lb, NI, u, tot, A.add, A.add)
+            yield ts(na_, u, v, tot, A.add, A.add)
+            ts(wa, la, u, BIG, A.is_ge, A.mult)
+            yield ts(wb, I, na_, BIG, A.is_ge, A.mult)
+            yield tt(ma, la, wa, A.add)
+        elif local_first:
+            ts(la, NI, tot, top, A.add, A.min)
+            ts(na_, u, v, tot, A.add, A.add)
+            yield ts(nv, tot, v, None, A.add)
+            ts(wa, I, nv, -BIG, A.is_ge, A.mult)
+            ts(lb, IM, nv, None, A.subtract)
+            yield ts(wb, I, na_, BIG, A.is_ge, A.mult)
+            yield tt(ma, la, wa, A.add)
+        else:
+            ts(wa, I, u if fline else v, BIG if fline else -BIG, A.is_ge, A.mult)
+            yield ts(wb, I, na_, BIG, A.is_ge, A.mult)
+            if fline:
+                ts(lb, NI, u, None, A.add)
+            else:
+                ts(lb, IM, v, top, A.subtract, A.min)
+            yield tt(ma, IM if fline else NI, wa, A.add)
+            yield 0
+        yield tt(mb, ma, lb, A.min if fline else A.max)
+        yield tt(fm, mb, wb, A.add)
+    far = lines()
+    last = [nc2]
+
+    def step():
+        vw("sv", last[0])
+        last[0] = next(far) or last[0]
+
+    step()
+    n = tr(T.tf[:], T.winf[:, 0:S_], nsc)
+    step()
+    n = tt(T.ya[:], T.tf[:, 0:S_:32], T.tf[:, 16:S_:32], A.max, n)
+    step()
+    n = tt(T.yb[L, :], T.ya[L, :], T.ya[U, :], A.max, n)
+    n = ts(T.yc[Q0, :], T.yb[Q1, :], float(HOP - VB), None, A.add, d=n)
+    step()
+    vw("sg", gyf)
+    tt(T.yf[Q0, 0:24], T.yb[Q0, :], T.yc[Q0, :], A.max, n)
+    n = tt(T.yf[Q0, 32:56], T.yb[Q0, :], T.yc[Q0, :], A.max)
+    step()
+    n = tr(T.ytf[Q0, :], T.yf[Q0, :], n)
+    tr(T.yff[Q0, 0:32], T.ytf[Q0, 0:64:2], n)
+    n = tr(T.yff[Q0, 32:64], T.ytf[Q0, 1:64:2])
+    if even:
+        nln = ts(nq, T.pt2[Q0, 31:32], ini2, 0.5, A.subtract, A.mult)
+    else:
+        nln = ts(nq, T.pt2[Q0, 63:64], T.pt2[Q0, 31:32], 0.5, A.subtract, A.mult)
+    n = tt(T.fl[Q0, :], T.yff[Q0, 0:56], fm, A.max, n)
+    for part in QS:
+        noff = ts(T.offf[part, :], T.fl[Q0, :], float(VB), float(ZC), A.add, A.min, d=n)
 
     def mm(bank, o, qb, sbuf, a, n):
         g.tensor.matmul_mx(T.ps[:, 512 * bank:512 * bank + n], T.wq[:, 128 * o:128 * o + 128], T.ws[:, 128 * o:128 * o + 128],
                            qb[:, a:a + n], sbuf[:, a:a + n], True, True).then_inc(s.st, 1)
         cnt["st"] += 1
     g.tensor.wait_ge(s.sv, nwq)
-    for bank, (qb, sbuf, a, n, sem, k) in enumerate(((T.xq, T.xs, 0, 512, None, 0), (T.xwq, T.xws, 0, 256, "aS0", 2 * ncp),
-                                                     (T.leq, T.les, 0, EARLY, "aE", 2 * nmf), (T.llq, T.lls, 0, 256, "aL", 2 * nmf))):
+    for bank, (qb, sbuf, n, sem, k) in enumerate(((T.xq, T.xs, T_, None, 0), (T.xwq, T.xws, C, "aS0", 2 * ncp),
+                                                  (T.leq, T.les, C, "aE", 2 * nmf), (T.llq, T.lls, C, "aL", 2 * nmf))):
         if sem:
             g.tensor.wait_ge(s[sem], k)
         for o in range(2):
-            mm(2 * bank + o, o, qb, sbuf, a, n)
-    res = (T.res0, T.res1)
-    base = (0, T_, FB, FB + EARLY)
-    width = (512, 256, EARLY, 256)
-    for b in range(3):
+            mm(2 * bank + o, o, qb, sbuf, 0, n)
+    res, yt = (T.res0, T.res1), (T.yt_0, T.yt_1)
+    for b, (base, width) in enumerate(((OWN, T_), (HOP, C), (0, C), (C, C))):
         for o in range(2):
+            if (b, o) == (3, 0):
+                nres0 = ncop
+                continue
             wait("a", g.scalar, "st", 2 * b + o + 1)
-            ncop = act(res[o][:, base[b]:base[b] + width[b]], T.ps[:, 512 * (2 * b + o):512 * (2 * b + o) + width[b]])
-    wait("a", g.scalar, "st", 8)
-    nlast = act(res[1][:, base[3]:base[3] + 256], T.ps[:, 512 * 7:512 * 7 + 256])
-    wait("v", g.vector, "st", 7)
-    n = cpy(res[0][:, base[3]:base[3] + 256], T.ps[:, 512 * 6:512 * 6 + 256])
-    g.vector.wait_ge(s.sg, 8)
-    g.scalar.wait_ge(s.sg, 8)
-    vsa(ncop)
-    for k in range(len(CUTS) - 1):
-        a, b = CUTS[k], CUTS[k + 1]
-        c = a // 16 + (8 if a >= S_ // 2 else 0)
-        of = T.offf[:, c:c + (b - a) // 16]
-        n0 = cpy(T.yt_0[:, a:b], T.res0[:].indirect(of), max(n, noff))
-        n1 = SA(lambda: g.scalar.activation(T.yt_1[:, a:b], T.res1[:].indirect(of), AF.Copy), noff, nlast)
-        if k == 0:
-            wait("s", g.sync, "sv", nln)
-            g.sync.dma_start(T.ln[:, :], T.lnt[0:1, :]).then_inc(s.yst, 16)
-        wait("s", g.sync, "sv", n0)
-        g.sync.dma_start(T.y[:, a:b], T.yt_0[:, a:b]).then_inc(s.yst, 16)
-        wait("s", g.sync, "sa", n1)
-        g.sync.dma_start(T.y[:, S_ + a:S_ + b], T.yt_1[:, a:b]).then_inc(s.yst, 16)
-    g.sync.wait_ge(s.yst, 16 * (2 * len(CUTS) - 1))
+            ncop = SA(lambda: g.scalar.activation(res[o][:, base:base + width],
+                                                  T.ps[:, 512 * (2 * b + o):512 * (2 * b + o) + width], AF.Copy))
+    vw("st", 7)
+    n0 = cpy(res[0][:, C:2 * C], T.ps[:, 512 * 6:512 * 6 + C])
+
+    def window(o, a, b):
+        c = a // 16 + (8 if a >= H else 0)
+        return res[o][:].indirect(T.offf[:, c:c + (b - a) // 16])
+
+    def vpick(o, a, b):
+        return cpy(yt[o][:, a:b], window(o, a, b), n0)
+
+    def spick(o, a, b):
+        return SA(lambda: g.scalar.activation(yt[o][:, a:b], window(o, a, b), AF.Copy), noff, ncop)
+
+    def store(o, a, b, v, a_=0):
+        wait("s", g.sync, "sv", v)
+        wait("s", g.sync, "sa", a_)
+        g.sync.dma_start(T.y[:, S_ * o + a:S_ * o + b], yt[o][:, a:b]).then_inc(s.yst, 16)
+
+    wait("s", g.sync, "sv", nln)
+    g.sync.dma_start(T.ln[:, :], lnv).then_inc(s.yst, 16)
+    vw("sg", gz)
+    wait("a", g.scalar, "sg", gz)
+    vw("sa", nres0)
+    store(0, 0, 128, vpick(0, 0, 128))
+    store(0, 128, H, vpick(0, 128, H))
+    store(1, 0, 128, 0, spick(1, 0, 128))
+    store(1, 128, H, 0, spick(1, 128, H))
+    store(0, H, S_, vpick(0, H, S_))
+    n1 = spick(1, H, 640)
+    vw("sa", ncop)
+    store(1, H, S_, vpick(1, 640, S_), n1)
+    g.sync.wait_ge(s.yst, 16 * 7)
     g.wait_ge(s.loc, cnt["loc"])

@@ -3,10 +3,10 @@ from concourse.mybir import dt, AluOpType, ActivationFunctionType
 
 T_, S_, C = 512, 768, 256
 H = S_ // 2
+NB = H // 16
 W0 = 2 * C
-D1, D2 = 1488, 800
+DUMP = 2048
 OWN, HOP, ZC = 2 * C, 2 * C + T_, 3 * C + T_
-VB = OWN + 256
 NONE = 4096.0
 BIG = 8192.0
 
@@ -25,21 +25,19 @@ SCRATCH = {
     "xwq": sb(2 * C, Q4), "xws": sb(2 * C, U8),
     "p0q": sb(C, Q4), "p0s": sb(C, U8), "peq": sb(C, Q4), "pes": sb(C, U8), "plq": sb(C, Q4), "pls": sb(C, U8),
     "leq": sb(C, Q4), "les": sb(C, U8), "llq": sb(C, Q4), "lls": sb(C, U8),
-    "pi": sb(2, I32), "pint": sb(2, I32), "pf": sb(2, F32), "one": sb(64, F32), "oneb": sb(C, BF), "d0": sb(32, F32),
-    "eqv": sb(1, F32), "sgn": sb(1, F32), "dmp": sb(1, F32), "ini": sb(1, F32), "sad": sb(1, F32), "k2": sb(8, F32),
-    "val0": sb(256, BF), "valb": sb(256, BF), "valc": sb(128, BF), "i0": sb(64, F32), "ii": sb(56, F32), "im": sb(56, F32),
-    "ni": sb(56, F32),
-    "t1": sb(32, I32), "z1": sb(32, F32), "x1": sb(64, F32), "xt1": sb(64, F32), "pt1": sb(32, F32), "a1": sb(32, F32),
-    "o1": sb(16, U16), "hm": sb(32, F32), "slu": sb(32, BF), "slin": sb(32, BF), "rx1": sb(64, F32), "ct1": sb(64, F32),
-    "winu": sb(D1 + 240, BF), "tu": sb(512, BF), "yu": sb(96, BF), "ytu": sb(64, BF), "yuu": sb(32, BF), "am": sb(16, BF),
-    "off0": sb(16, U16), "offe": sb(16, U16), "offl": sb(16, U16),
+    "pi": sb(2, I32), "pint": sb(4, I32), "pf": sb(4, F32), "one": sb(64, F32), "two": sb(32, F32), "d0": sb(32, F32),
+    "eqv": sb(1, F32), "sgn": sb(1, F32), "ini": sb(1, F32), "k2": sb(4, F32), "dt0": sb(48, F32), "dtl": sb(48, F32),
+    "val": sb(256, BF), "ramp": sb(C, BF), "valc": sb(128, BF), "i0": sb(NB, F32), "ii": sb(NB, F32), "ni": sb(NB, F32),
+    "t1": sb(32, I32), "z1": sb(32, F32), "m1": sb(16, F32), "x1": sb(64, F32), "xt1": sb(64, F32), "pt1": sb(32, F32), "a1": sb(32, F32),
+    "o1": sb(16, U16), "hm": sb(32, BF), "slu": sb(32, BF), "slin": sb(32, BF), "rx1": sb(64, F32), "ct1": sb(64, F32),
+    "winu": sb(DUMP + 256, BF), "tu": sb(512, BF), "yu": sb(64, U16), "ytu": sb(64, U16),
+    "off0": sb(32, U16), "offe": sb(32, U16), "offl": sb(32, U16),
     "cf": sb(4, F32), "cg": sb(4, F32), "sc": sb(8, F32),
-    "t2": sb(64, I32), "z2": sb(66, BF), "x2": sb(128, BF), "xt2": sb(128, BF), "pt2": sb(64, F32), "w2": sb(48, F32),
-    "y2": sb(48, F32), "a2": sb(48, F32), "o2": sb(8, U16), "rx2": sb(32, F32), "ct2": sb(40, F32),
-    "winf": sb(D2 + 240, BF), "tf": sb(S_, BF), "ya": sb(24, F32), "yb": sb(24, F32), "yc": sb(24, F32), "yf": sb(64, F32),
-    "ytf": sb(64, F32), "yff": sb(64, F32),
-    "la": sb(56, F32), "lb": sb(56, F32), "wa": sb(56, F32), "wb": sb(56, F32), "ma": sb(56, F32), "mb": sb(56, F32),
-    "fm": sb(56, F32), "fl": sb(56, F32), "offf": sb(56, U16),
+    "t2": sb(64, I32), "z2": sb(66, BF), "m2": sb(48, F32), "x2": sb(128, BF), "xt2": sb(128, BF), "pt2": sb(64, F32),
+    "w2": sb(48, F32), "y2": sb(48, F32), "o2": sb(8, U16), "rx2": sb(32, F32), "ct2": sb(40, F32),
+    "winf": sb(DUMP + 256, BF), "tf": sb(S_, BF), "ya": sb(5 * NB, F32), "yd": sb(5 * NB, F32), "ys": sb(160, U16),
+    "ytf": sb(64, U16), "offf": sb(64, U16),
+    "la": sb(NB, F32), "lb": sb(NB, F32), "wa": sb(NB, F32), "wb": sb(NB, F32), "ma": sb(NB, F32), "mb": sb(NB, F32),
     "res0": sb(ZC + 8, F32), "res1": sb(ZC + 8, F32), "yt_0": sb(S_, F32), "yt_1": sb(S_, F32),
     "ps": ("psum", [128, 4096], F32),
 }
@@ -104,8 +102,8 @@ def rank_program(g, core, T, topo):
     def tr(out, in_, d=0):
         return V(lambda: g.vector.transpose(out, in_), d)
 
-    def scan(out, d0, d1, init, d=0):
-        return V(lambda: g.vector.tensor_tensor_scan(out, d0, d1, init, A.mult, A.add), d)
+    def scan(out, d0, d1, init, d=0, op0=A.mult, op1=A.add):
+        return V(lambda: g.vector.tensor_tensor_scan(out, d0, d1, init, op0, op1), d)
 
     def fill(ap, c, d=0):
         return V(lambda: g.vector.memset(ap, c), d)
@@ -113,8 +111,8 @@ def rank_program(g, core, T, topo):
     def quant(qb, sbuf, src, a):
         return V(lambda: g.vector.quantize_mx(qb[:, a:a + 128], sbuf[:, a:a + 128], src[:, 4 * a:4 * a + 512]))
 
-    def spread(off, src, d=0):
-        return [ts(off[part, :], src, 256.0, None, A.add, d=d) for part in QS][-1]
+    def spread(off, c, src, d=0):
+        return [tr(off[part, c:c + 32], src, d) for part in QS][-1]
 
     def iota(out, pattern, base, cm=0, whole=False):
         kw = {} if whole else {"allow_small_or_imprecise_dtypes": True}
@@ -149,25 +147,27 @@ def rank_program(g, core, T, topo):
     ob = 0 if even else 32
     ndm2 = fill(T.dm2[:, ob:ob + 32], 0)
     fill(T.dmt[G0, 0:4], 0)
-    fill(T.winu[:, W0:2 * W0], -NONE)
-    nwu = fill(T.oneb[U, :], 1.0)
+    fill(T.winu[:, W0 + 1:2 * W0:2], 0.0)
+    fill(T.one[:], 1.0)
     gpi = iota(T.pi[:, 0:1], [[1, 1]], 0, 1, whole=True)
     vw("sg", gpi)
-    ts(T.pint[:, 0:1], T.pi[:, 0:1], 16, None, A.bitwise_and)
-    n = ts(T.pint[:, 1:2], T.pi[:, 0:1], 15, None, A.bitwise_and)
-    fill(T.one[:], 1.0)
+    for j, m in enumerate((16, 15, 30, 1)):
+        n = ts(T.pint[:, j:j + 1], T.pi[:, 0:1], m, None, A.bitwise_and)
     for part, c in ((Q0, G), (Q1, P), (U, Fb)):
         fill(T.eqv[part, :], float(c))
-    ts(T.pf[:, 0:1], T.pint[:, 0:1], 16.0, None, A.mult, d=n)
-    npf = cpy(T.pf[:, 1:2], T.pint[:, 1:2])
-    h16, s16 = T.pf[:, 0:1], T.pf[:, 1:2]
-    scan(T.winu[U, W0:2 * W0:2], T.oneb[U, :], T.oneb[U, :], -257.0)
     for part, c in ((Q0, -2.0), (Q1, 2.0), (U, 2.0)):
         fill(T.sgn[part, :], c)
-    line(T.dmp[:], s16, 16.0, float(D1), npf)
-    ts(T.d0[:], T.one[:, 0:32], h16, None, A.is_gt)
+    for j, c in enumerate((16.0, 1.0, 0.5, float(H))):
+        npf = ts(T.pf[:, j:j + 1], T.pint[:, j:j + 1], c, None, A.mult, d=n)
+    h256, s16 = T.pf[:, 0:1], T.pf[:, 1:2]
     for part, c in ((Q0, 2 * W0), (Q1, W0 - 2), (Q2, W0 - 2), (Q3, -2)):
-        nk = line(T.ini[part, :], T.pf[part, 1:2], -1.0, c + 16.0)
+        fill(T.ini[part, :], float(c))
+    fill(T.k2[0:96, 0:1], 0.0)
+    fill(T.two[Q0, :], 2.0)
+    ts(T.d0[:], T.one[:, 0:32], h256, None, A.is_gt, d=npf)
+    ts(T.k2[Q3, 0:1], T.pf[Q3, 0:1], 1.0 / 256, None, A.mult)
+    line(T.k2[:, 1:2], h256, -1.0, 256.0)
+    nk = ts(T.k2[:, 2:3], h256, -256.0, None, A.add)
 
     g.sync.dma_start(T.dmt[0:16, 4:36], T.dm[:, :]).then_inc(s.dml, 16)
     g.scalar.dma_start(T.dmt[16:32, 3:35], T.dm[:, :]).then_inc(s.dml, 16)
@@ -178,53 +178,56 @@ def rank_program(g, core, T, topo):
     g.sync.dma_start(T.xt[:, 1024:2048], T.x[:, 1024:2048]).then_inc(s.xl1, 16)
     g.scalar.dma_start(T.wt[:], T.w[:]).then_inc(s.wl, 16)
 
-    gval = iota(T.val0[:], [[1, 16], [16, 16]], -256)
-    gi0 = iota(T.i0[Q0, :], [[H, 2], [16, 32]], 0)
+    gdt = iota(T.dt0[:], [[0, 3], [16, 16]], DUMP)
+    gramp = iota(T.ramp[:], [[1, C]], -C)
     g.wait_ge(s.dm2, 32)
     send(cp, T.dm2[:, ob:ob + 32], T.dm2[:, ob:ob + 32], "aDM")
-    gyu = iota(T.yu[:], [[0, 96]], 0)
-    gyf = iota(T.yf[Q0, :], [[0, 64]], 0)
-    for b in (T.res0, T.res1):
-        gz = iota(b[:, ZC:ZC + 8], [[0, 8]], 0)
+    gval = iota(T.val[:], [[1, 16], [16, 16]], 0)
+    gi0 = iota(T.i0[Q0, :], [[16, NB]], 0)
+    ghm = iota(T.hm[:], [[0, 32]], 0)
 
-    s0 = T.pf[Q0, 1:2]
-    kini, kthr, kdmp, ksl = (T.k2[Q0, j:j + 1] for j in range(4))
-    I, IM, NI = T.ii[Q0, :], T.im[Q0, :], T.ni[Q0, :]
-    sh = VB if local_first and fline else 0
+    I, NI = T.ii[Q0, :], T.ni[Q0, :]
     g.vector.wait_ge(s.dml, 32)
     for part, m in ((Q0, G), (Q1, P | G), (Q2, Fb), (Q3, Fb)):
         n = ts(T.t1[part, :], T.dmt[Q0, 3:35], m, None, A.bitwise_and)
-    ts(T.sad[:], s16, -16.0, None, A.add)
-    line(kini, s0, -1.0, 14.0 if local_first else 16.0 + W0)
-    line(kthr, s0, -1.0, S_ + 16.0)
-    line(kdmp, s0, 16.0, float(D2))
-    n = ts(T.z1[:], T.t1[:], T.eqv[:], T.sgn[:], A.is_equal, A.mult, d=n)
-    ts(T.x1[:, 32:64], T.t1[:], T.eqv[:], T.dmp[:], A.not_equal, A.mult)
-    vw("sg", gval)
-    nval = ts(T.valb[:], T.val0[:], h16, None, A.add)
-    n = scan(T.x1[:, 0:32], T.d0[:], T.z1[:], 0.0, n)
-    line(ksl, s0, 0.5, -(W0 + 16) / 2)
+    vw("sg", gdt)
+    ts(T.dtl[:], T.dt0[:], s16, None, A.add)
+    fill(T.yu[:], 0)
     fill(T.z2[G0, 0:1], 0.0)
-    vw("sg", gi0)
-    nii = ts(I, T.i0[Q0, 0:56], s0, None, A.add)
+    n = ts(T.z1[:], T.t1[:], T.eqv[:], T.sgn[:], A.is_equal, A.mult, d=n)
+    ts(T.x1[:, 32:64], T.t1[:], T.eqv[:], None, A.not_equal)
+    vw("sg", gramp)
+    ts(T.winu[:, W0:2 * W0:2], T.ramp[:], T.k2[:, 0:1], T.k2[:, 1:2], A.mult, A.add)
+    n = scan(T.x1[:, 0:32], T.d0[:], T.z1[:], 0.0, n)
+    for j, c in enumerate((-BIG, 0.0, float(HOP - OWN - 256), 0.0, float(OWN + 256))):
+        fill(T.yd[Q0, j:5 * NB:5], c)
     n = tr(T.xt1[:], T.x1[:], n)
-    cpy(T.valc[L, :], T.valb[L, 0:128], nval)
-    nvc = cpy(T.valc[U, :], T.valb[U, 128:256])
-    npt = scan(T.pt1[:], T.one[:, 0:32], T.xt1[:, 0:32], T.ini[:], n)
     g.vector.wait_ge(s.xl0, 16)
     quant(T.xq, T.xs, T.xt, 0)
-    na1 = tt(T.a1[:, 16:32], T.pt1[:, 16:32], T.xt1[:, 48:64], A.max, npt)
+    scan(T.pt1[:], T.one[:, 0:32], T.xt1[:, 0:32], T.ini[:], n)
+    npt = tt(T.m1[:], T.xt1[:, 48:64], T.dtl[:, 0:16], A.mult)
+    quant(T.xq, T.xs, T.xt, 128)
+    tt(T.a1[Q0, 0:16], T.pt1[Q0, 16:32], T.m1[Q0, :], A.max, npt)
+    n = tt(T.a1[Q0, 16:32], T.pt1[Q1, 16:32], T.m1[Q1, :], A.max)
+    for part in (Q1, U):
+        tt(T.o1[part, :], T.pt1[part, 16:32], T.m1[part, :], A.max)
     for o_, c, i_ in ((L, 0, L), (U, 0, L), (L, 32, U), (U, 32, U)):
         nrx = ts(T.rx1[o_, c:c + 32], T.one[i_, 0:32], T.pt1[i_, 31:32], None, A.mult)
-    line(NI, I, -1.0, 2 * C - 1.0 - VB + sh, nii)
-    n = ts(T.o1[:], T.a1[:, 16:32], T.sad[:], None, A.add, d=na1)
-    nct = tr(T.ct1[:], T.rx1[:], nrx)
-    for c, part in ((0, Q0), (16, Q1)):
-        nhm = ts(T.hm[Q0, c:c + 16], T.a1[part, 16:32], 0.5, None, A.mult)
-    nwin = cpy(T.winu[:].indirect(T.o1[:]), T.valb[:], n)
+    no1 = tt(T.o1[Q0, :], T.a1[Q0, 0:16], T.a1[Q0, 16:32], A.min, n)
+    g.vector.wait_ge(s.xl1, 16)
+    quant(T.xq, T.xs, T.xt, 256)
+    vw("sg", gval)
+    nwin = cpy(T.winu[:].indirect(T.o1[:]), T.val[:], no1)
+    nct = tr(T.ct1[:], T.rx1[:])
+    vw("sg", ghm)
+    nhm = ts(T.hm[Q0, 16:32], T.o1[Q0, :], -float(W0), 0.5, A.add, A.mult)
+    quant(T.xq, T.xs, T.xt, 384)
 
     g.scalar.wait_ge(s.xl0, 16)
     nwf = SA(lambda: g.scalar.activation(T.winf[:, 0:S_], T.xt[:, 0:S_], AF.Identity, scale=0.0, bias=-NONE))
+    wait("a", g.scalar, "sg", gval)
+    for part, c in ((L, 0), (U, 128)):
+        nvc = SA(lambda: g.scalar.activation(T.valc[part, :], T.val[part, c:c + 128], AF.Identity, bias=T.k2[part, 2:3]), nk)
     wait("g", g, "sv", nct)
     trs = []
     for dst, land, h in ((cg_, T.cg, 0), (cf_, T.cf, 1)):
@@ -236,114 +239,100 @@ def rank_program(g, core, T, topo):
         cnt["loc"] += len(en)
     g.remote_dma_fused(trs, local_sem=s.loc)
 
-    nhm = tt(T.hm[Q0, 16:32], T.hm[Q0, 0:16], T.hm[Q0, 16:32], A.min, nhm)
-    quant(T.xq, T.xs, T.xt, 128)
     n = tr(T.tu[:], T.winu[:, W0:2 * W0], nwin)
-    vw("sg", gyu)
-    nhm = ts(T.yu[Q0, 80:96], T.hm[Q0, 16:32], ksl, None, A.add, d=nhm)
+    nslu = tr(T.slu[:], T.hm[:], nhm)
     g.vector.wait_ge(s.aDM, ncp)
     g.vector.wait_ge(s.dm2, 32)
     n2 = ts(T.t2[Q0, :], T.dm2[Q0, :], Qb, None, A.bitwise_and)
-    ts(IM, I, -float(VB), None, A.add)
-    tt(T.yu[:, 0:16], T.tu[:, 0:512:32], T.tu[:, 16:512:32], A.max, n)
-    n = tt(T.yu[:, 32:48], T.tu[:, 0:512:32], T.tu[:, 16:512:32], A.max)
-    nslu = tr(T.slu[:], T.yu[:, 64:96], nhm)
-    g.vector.wait_ge(s.xl1, 16)
-    quant(T.xq, T.xs, T.xt, 256)
-    n = tr(T.ytu[:], T.yu[:, 0:64], n)
+    g.vector.wait_ge(s.wl, 16)
+    quant(T.wq, T.ws, T.wt, 0)
+    tt(T.yu[:, 0:16], T.tu[:, 0:512:32], T.tu[:, 16:512:32], A.add, n)
+    n = tt(T.yu[:, 32:48], T.tu[:, 0:512:32], T.tu[:, 16:512:32], A.add)
+    nwq = quant(T.wq, T.ws, T.wt, 128)
+    n = tr(T.ytu[:], T.yu[:], n)
     ts(T.z2[G0, 1:65], T.t2[G0, :], 0.0, 2.0, A.is_gt, A.mult, d=n2)
-    ts(T.x2[Q0, 64:128], T.t2[Q0, :], 0.0, kdmp, A.is_equal, A.mult)
+    ts(T.x2[Q0, 64:128], T.t2[Q0, :], 0.0, None, A.is_equal)
     n2 = ts(T.x2[Q0, 0:64], T.t2[Q0, :], 0.0, 2.0, A.is_gt, A.mult)
-    ny = tr(T.yuu[:], T.ytu[:, 0:64:2], n)
-    quant(T.xq, T.xs, T.xt, 384)
+    n0 = spread(T.off0, 0, T.ytu[Q0, 0:64:2], n)
+    ne = spread(T.offe, 0, T.ytu[Q2, 0:64:2])
     n2 = scan(T.x2[G0, 0:64], T.one[G0, :], T.z2[G0, 0:64], 0.0, n2)
-    n = tt(T.am[Q0, :], T.yuu[Q0, 0:16], T.yuu[Q1, 0:16], A.max, ny)
-    n0 = spread(T.off0, T.am[Q0, :], n)
+    p0 = pick(T.p0q[:], T.p0s[:], T.xq[:], T.xs[:], T.off0[:, 0:16], n0)
     n2 = tr(T.xt2[Q0, :], T.x2[Q0, :], n2)
-    u, v, ini2, nv = (T.sc[Q0, j:j + 1] for j in range(4))
-    if local_first:
-        ini2 = kini
-    else:
-        g.vector.wait_ge(s.aCNT, nmf)
-        n2 = ts(ini2, kini, T.cf[Q0, 3:4], T.cg[Q0, 3:4], A.add, A.subtract)
-    ne = spread(T.offe, T.yuu[Q2, 0:16])
-    p0 = pick(T.p0q[:], T.p0s[:], T.xq[:], T.xs[:], T.off0[:], n0)
-    scan(T.pt2[Q0, 0:32], T.one[Q0, 0:32], T.xt2[Q0, 0:32], ini2, n2)
-    n2 = scan(T.pt2[Q0, 32:64], T.one[Q0, 0:32], T.xt2[Q0, 32:64], ini2)
-    pe = pick(T.peq[:], T.pes[:], T.xq[:], T.xs[:], T.offe[:], ne)
+    pe = pick(T.peq[:], T.pes[:], T.xq[:], T.xs[:], T.offe[:, 0:16], ne)
 
     wait("g", g, "sv", nslu)
     send(cp, T.slin[:], T.slu[:], "aSL")
+    for b in (T.res0, T.res1):
+        gz = iota(b[:, ZC:ZC + 8], [[0, 8]], 0)
     send_pick(cp, T.xwq[:, 0:C], T.xws[:, 0:C], T.p0q[:], T.p0s[:], p0, "aS0")
     send_pick(cf_, T.leq[:], T.les[:], T.peq[:], T.pes[:], pe, "aE")
     g.sync.wait_ge(s.aSL, ncp)
-    wait("s", g.sync, "sv", nvc)
+    wait("s", g.sync, "sa", nvc)
     for k in range(4):
         a, r, h = 32 + 64 * (k // 2) + 16 * (k % 2), 16 + 8 * (k // 2), 16 * (k % 2)
         g.sync.dma_start(T.valc[a:a + 1, :], T.slin[r:r + 8, h:h + 16]).then_inc(s.vps, 16)
 
-    nw = ts(T.w2[Q0, :], T.pt2[Q0, 16:64], kthr, 1.0 - S_, A.is_ge, A.mult, d=n2)
-    nrx = ts(T.rx2[Q0, :], T.one[Q0, 0:32], T.pt2[Q0, 63:64], 0.5, A.add, A.mult)
-    g.vector.wait_ge(s.wl, 16)
-    quant(T.wq, T.ws, T.wt, 0)
-    n = tt(T.y2[Q0, :], T.pt2[Q0, 16:64], T.w2[Q0, :], A.add, nw)
-    nc2 = tr(T.ct2[Q0, 0:32], T.rx2[Q0, :], nrx)
-    nwq = quant(T.wq, T.ws, T.wt, 128)
-    n = tt(T.a2[Q0, :], T.y2[Q0, :], T.xt2[Q0, 80:128], A.max, n)
+    u, v, ini2, nv = (T.sc[Q0, j:j + 1] for j in range(4))
+    g.vector.wait_ge(s.aCNT, nmf)
+    n = n2
+    if local_first:
+        ini2 = -2.0
+    else:
+        n = ts(ini2, T.cf[Q0, 3:4], T.cg[Q0, 3:4], float(W0), A.subtract, A.add)
+    tt(T.m2[Q0, :], T.xt2[Q0, 80:128], T.dtl[Q0, :], A.mult, n2)
+    scan(T.pt2[Q0, 0:32], T.one[Q0, 0:32], T.xt2[Q0, 0:32], ini2, n)
+    n = scan(T.pt2[Q0, 32:64], T.one[Q0, 0:32], T.xt2[Q0, 32:64], ini2)
     quant(T.xwq, T.xws, T.xt, C)
-    spread(T.offl, T.yuu[Q3, 0:16])
-    nxw = quant(T.xwq, T.xws, T.xt, C + 128)
+    vw("sg", gi0)
+    nii = ts(I, T.i0[Q0, :], T.pf[Q0, 2:3], T.pf[Q0, 3:4], A.add, A.add)
+    nw = ts(T.w2[Q0, :], T.pt2[Q0, 16:64], float(S_), 1.0 - S_, A.is_ge, A.mult, d=n)
+    nrx = ts(T.rx2[Q0, :], T.two[Q0, :], T.pt2[Q0, 63:64], 0.5, A.add, A.mult)
+    quant(T.xwq, T.xws, T.xt, C + 128)
+    n = tt(T.y2[Q0, :], T.pt2[Q0, 16:64], T.w2[Q0, :], A.add, nw)
+    nxw = spread(T.offl, 0, T.ytu[Q3, 0:64:2])
+    tr(T.ct2[Q0, 0:32], T.rx2[Q0, :], nrx)
+    line(NI, I, -1.0, OWN - 1.0)
+    line(u, T.cf[Q0, 3:4], 0.5, 1.0 - C)
+    nc2 = line(v, T.cg[Q0, 3:4], -0.5, float(W0))
     oc, pc = (0, 32) if even else (32, 0)
     for part, c in ((Q0, oc), (Q1, pc), (Q2, oc + 8), (Q3, pc + 8)):
-        no2 = ts(T.o2[part, :], T.a2[Q0, c:c + 8], T.sad[Q0, :], None, A.add, d=n)
-    if local_first:
-        g.vector.wait_ge(s.aCNT, nmf)
-    line(u, T.cf[Q0, 3:4], 0.5, -(W0 - 1) / 2 - sh)
-    nc2 = line(v, T.cg[Q0, 3:4], -0.5, (2 * W0 + 1) / 2 + sh)
-
-    g.vector.wait_ge(s.aS0, 2 * ncp)
-    g.scalar.wait_ge(s.aS0, 2 * ncp)
-    pl = pick(T.plq[:], T.pls[:], T.xwq[:], T.xws[:], T.offl[:], nxw)
-    send_pick(cf_, T.llq[:], T.lls[:], T.plq[:], T.pls[:], pl, "aL")
-    g.vector.wait_ge(s.vps, 64)
-    vw("sa", nwf)
-    nsc = cpy(T.winf[:].indirect(T.o2[:]), T.valc[:], no2)
+        no2 = tt(T.o2[part, :], T.y2[Q0, c:c + 8], T.m2[Q0, c:c + 8], A.max, n)
+    fill(T.ys[Q0, :], 0)
 
     tot = T.ct2[Q0, 31:32]
     if local_first:
         na_, nq, lnv = T.ct2[Q0, 32:33], T.ct2[Q0, 33:34], T.ct2[31:32, 32:34]
     else:
         na_, nq, lnv = tot, T.ct2[Q0, 32:33], T.ct2[31:32, 31:33]
-    la, lb, wa, wb, ma, mb, fm = (t[Q0, :] for t in (T.la, T.lb, T.wa, T.wb, T.ma, T.mb, T.fm))
-    top = 2 * C - 1.0 - VB
+    la, lb, wa, wb, ma, mb = (t[Q0, :] for t in (T.la, T.lb, T.wa, T.wb, T.ma, T.mb))
 
     def lines():
         if local_first and fline:
-            ts(la, I, tot, -float(VB), A.subtract, A.add)
+            ts(la, I, tot, None, A.subtract)
             ts(lb, NI, u, tot, A.add, A.add)
             yield ts(na_, u, v, tot, A.add, A.add)
             ts(wa, la, u, BIG, A.is_ge, A.mult)
-            yield ts(wb, I, na_, BIG, A.is_ge, A.mult)
+            yield ts(wb, I, na_, float(ZC), A.is_ge, A.mult)
             yield tt(ma, la, wa, A.add)
         elif local_first:
-            ts(la, NI, tot, top, A.add, A.min)
+            ts(la, NI, tot, OWN - 1.0, A.add, A.min)
             ts(na_, u, v, tot, A.add, A.add)
             yield ts(nv, tot, v, None, A.add)
             ts(wa, I, nv, -BIG, A.is_ge, A.mult)
-            ts(lb, IM, nv, None, A.subtract)
-            yield ts(wb, I, na_, BIG, A.is_ge, A.mult)
+            ts(lb, I, nv, None, A.subtract)
+            yield ts(wb, I, na_, float(ZC), A.is_ge, A.mult)
             yield tt(ma, la, wa, A.add)
         else:
             ts(wa, I, u if fline else v, BIG if fline else -BIG, A.is_ge, A.mult)
-            yield ts(wb, I, na_, BIG, A.is_ge, A.mult)
+            yield ts(wb, I, na_, float(ZC), A.is_ge, A.mult)
             if fline:
                 ts(lb, NI, u, None, A.add)
             else:
-                ts(lb, IM, v, top, A.subtract, A.min)
-            yield tt(ma, IM if fline else NI, wa, A.add)
+                ts(lb, I, v, OWN - 1.0, A.subtract, A.min)
+            yield tt(ma, I if fline else NI, wa, A.add)
             yield 0
         yield tt(mb, ma, lb, A.min if fline else A.max)
-        yield tt(fm, mb, wb, A.add)
+        yield tt(T.ya[Q0, 4:5 * NB:5], mb, wb, A.max)
     far = lines()
     last = [nc2]
 
@@ -351,28 +340,40 @@ def rank_program(g, core, T, topo):
         vw("sv", last[0])
         last[0] = next(far) or last[0]
 
+    res, yt = (T.res0, T.res1), (T.yt_0, T.yt_1)
+
+    def results(b, o):
+        base, width = ((OWN, T_), (HOP, C), (0, C), (C, C))[b]
+        wait("a", g.scalar, "st", 2 * b + o + 1)
+        return SA(lambda: g.scalar.activation(res[o][:, base:base + width],
+                                              T.ps[:, 512 * (2 * b + o):512 * (2 * b + o) + width], AF.Copy))
     step()
-    n = tr(T.tf[:], T.winf[:, 0:S_], nsc)
+    results(0, 0)
+    results(0, 1)
+    g.vector.wait_ge(s.aS0, 2 * ncp)
+    g.scalar.wait_ge(s.aS0, 2 * ncp)
+    pl = pick(T.plq[:], T.pls[:], T.xwq[:], T.xws[:], T.offl[:, 0:16], nxw)
+    send_pick(cf_, T.llq[:], T.lls[:], T.plq[:], T.pls[:], pl, "aL")
+
     step()
-    n = tt(T.ya[:], T.tf[:, 0:S_:32], T.tf[:, 16:S_:32], A.max, n)
+    g.vector.wait_ge(s.vps, 64)
+    vw("sa", nvc)
+    n = cpy(T.winf[:].indirect(T.o2[:]), T.valc[:], no2)
     step()
-    n = tt(T.yb[L, :], T.ya[L, :], T.ya[U, :], A.max, n)
-    n = ts(T.yc[Q0, :], T.yb[Q1, :], float(HOP - VB), None, A.add, d=n)
+    n = tr(T.tf[:], T.winf[:, 0:S_], n)
     step()
-    vw("sg", gyf)
-    tt(T.yf[Q0, 0:24], T.yb[Q0, :], T.yc[Q0, :], A.max, n)
-    n = tt(T.yf[Q0, 32:56], T.yb[Q0, :], T.yc[Q0, :], A.max)
+    for j, part in enumerate((Q1, Q3, Q0, Q2)):
+        tt(T.ya[Q0, j:5 * NB:5], T.tf[part, 0:S_:32], T.tf[part, 16:S_:32], A.max, n)
     step()
-    n = tr(T.ytf[Q0, :], T.yf[Q0, :], n)
-    tr(T.yff[Q0, 0:32], T.ytf[Q0, 0:64:2], n)
-    n = tr(T.yff[Q0, 32:64], T.ytf[Q0, 1:64:2])
+    n = scan(T.ys[Q0, 0:5 * NB], T.yd[Q0, :], T.ya[Q0, :], 0.0, last[0], A.add, A.max)
     if even:
         nln = ts(nq, T.pt2[Q0, 31:32], ini2, 0.5, A.subtract, A.mult)
     else:
         nln = ts(nq, T.pt2[Q0, 63:64], T.pt2[Q0, 31:32], 0.5, A.subtract, A.mult)
-    n = tt(T.fl[Q0, :], T.yff[Q0, 0:56], fm, A.max, n)
-    for part in QS:
-        noff = ts(T.offf[part, :], T.fl[Q0, :], float(VB), float(ZC), A.add, A.min, d=n)
+    tr(T.ytf[Q0, 0:32], T.ys[Q0, 4:160:5], n)
+    n = tr(T.ytf[Q0, 32:64], T.ys[Q0, 4:160:5])
+    spread(T.offf, 0, T.ytf[Q0, 0:64:2], n)
+    noff = spread(T.offf, 32, T.ytf[Q0, 1:64:2])
 
     def mm(bank, o, qb, sbuf, a, n):
         g.tensor.matmul_mx(T.ps[:, 512 * bank:512 * bank + n], T.wq[:, 128 * o:128 * o + 128], T.ws[:, 128 * o:128 * o + 128],
@@ -385,15 +386,9 @@ def rank_program(g, core, T, topo):
             g.tensor.wait_ge(s[sem], k)
         for o in range(2):
             mm(2 * bank + o, o, qb, sbuf, 0, n)
-    res, yt = (T.res0, T.res1), (T.yt_0, T.yt_1)
-    for b, (base, width) in enumerate(((OWN, T_), (HOP, C), (0, C), (C, C))):
-        for o in range(2):
-            if (b, o) == (3, 0):
-                nres0 = ncop
-                continue
-            wait("a", g.scalar, "st", 2 * b + o + 1)
-            ncop = SA(lambda: g.scalar.activation(res[o][:, base:base + width],
-                                                  T.ps[:, 512 * (2 * b + o):512 * (2 * b + o) + width], AF.Copy))
+    for b, o in ((1, 0), (1, 1), (2, 0), (2, 1)):
+        nres0 = results(b, o)
+    ncop = results(3, 1)
     vw("st", 7)
     n0 = cpy(res[0][:, C:2 * C], T.ps[:, 512 * 6:512 * 6 + C])
 

@@ -4,9 +4,12 @@ from concourse.mybir import dt, AluOpType, ActivationFunctionType
 T_, S_, C = 512, 768, 256
 H = S_ // 2
 NB = H // 16
+NY = 6 * NB
 W0 = 2 * C
 DUMP = 2048
-OWN, HOP, ZC = 2 * C, 2 * C + T_, 3 * C + T_
+E, LT = 256, 224
+B = C - LT
+OWN, HOP, ZC = E + C, E + C + T_, E + 2 * C + T_
 NONE = 4096.0
 BIG = 8192.0
 
@@ -22,27 +25,29 @@ SCRATCH = {
     "dmt": sb(36, I32), "dm2": sb(64, I32),
     "xt": sb(2048, BF), "wt": sb(1024, BF),
     "xq": sb(T_, Q4), "xs": sb(T_, U8), "wq": sb(256, Q4), "ws": sb(256, U8),
-    "xwq": sb(2 * C, Q4), "xws": sb(2 * C, U8),
-    "p0q": sb(C, Q4), "p0s": sb(C, U8), "peq": sb(C, Q4), "pes": sb(C, U8), "plq": sb(C, Q4), "pls": sb(C, U8),
-    "leq": sb(C, Q4), "les": sb(C, U8), "llq": sb(C, Q4), "lls": sb(C, U8),
-    "pi": sb(2, I32), "pint": sb(4, I32), "pf": sb(4, F32), "one": sb(64, F32), "two": sb(32, F32), "d0": sb(32, F32),
+    "xwq": sb(T_, Q4), "xws": sb(T_, U8),
+    "p0q": sb(C, Q4), "p0s": sb(C, U8), "peq": sb(E, Q4), "pes": sb(E, U8), "plq": sb(C, Q4), "pls": sb(LT + 4 * B, U8),
+    "leq": sb(E, Q4), "les": sb(E, U8), "llq": sb(C, Q4), "lls": sb(C, U8),
+    "pi": sb(2, I32), "pint": sb(4, I32), "pf": sb(6, F32), "one": sb(64, F32), "two": sb(32, F32), "hs": sb(32, F32), "d0": sb(32, F32),
     "eqv": sb(1, F32), "sgn": sb(1, F32), "ini": sb(1, F32), "k2": sb(4, F32), "dt0": sb(48, F32), "dtl": sb(48, F32),
-    "val": sb(256, BF), "ramp": sb(C, BF), "valc": sb(128, BF), "i0": sb(NB, F32), "ii": sb(NB, F32), "ni": sb(NB, F32),
-    "t1": sb(32, I32), "z1": sb(32, F32), "m1": sb(16, F32), "x1": sb(64, F32), "xt1": sb(64, F32), "pt1": sb(32, F32), "a1": sb(32, F32),
-    "o1": sb(16, U16), "hm": sb(32, BF), "slu": sb(32, BF), "slin": sb(32, BF), "rx1": sb(64, F32), "ct1": sb(64, F32),
+    "val": sb(256, BF), "valc": sb(128, BF), "i0": sb(NB, F32), "ii": sb(NB, F32), "ni": sb(NB, F32),
+    "t1": sb(32, I32), "z1": sb(32, F32), "x1": sb(64, F32), "xt1": sb(64, F32), "pt1": sb(32, F32), "m1": sb(16, F32),
+    "a1": sb(32, F32), "o1": sb(16, U16), "ramp": sb(C, BF), "hm": sb(32, BF), "msg": sb(32, BF), "msi": sb(32, BF),
+    "rx1": sb(64, F32), "ct1": sb(64, F32),
     "winu": sb(DUMP + 256, BF), "tu": sb(512, BF), "yu": sb(64, U16), "ytu": sb(64, U16),
-    "off0": sb(32, U16), "offe": sb(32, U16), "offl": sb(32, U16),
-    "cf": sb(4, F32), "cg": sb(4, F32), "sc": sb(8, F32),
-    "t2": sb(64, I32), "z2": sb(66, BF), "m2": sb(48, F32), "x2": sb(128, BF), "xt2": sb(128, BF), "pt2": sb(64, F32),
+    "off0": sb(32, U16), "offe": sb(32, U16),
+    "cf": sb(1, F32), "cg": sb(1, F32), "sc": sb(8, F32),
+    "t2": sb(64, I32), "z2": sb(66, BF), "x2": sb(128, BF), "xt2": sb(128, BF), "pt2": sb(64, F32),
+    "pr2": sb(64, F32), "top": sb(1, F32), "m2": sb(48, F32),
     "w2": sb(48, F32), "y2": sb(48, F32), "o2": sb(8, U16), "rx2": sb(32, F32), "ct2": sb(40, F32),
-    "winf": sb(DUMP + 256, BF), "tf": sb(S_, BF), "ya": sb(5 * NB, F32), "yd": sb(5 * NB, F32), "ys": sb(160, U16),
-    "ytf": sb(64, U16), "offf": sb(64, U16),
-    "la": sb(NB, F32), "lb": sb(NB, F32), "wa": sb(NB, F32), "wb": sb(NB, F32), "ma": sb(NB, F32), "mb": sb(NB, F32),
+    "winf": sb(DUMP + 256, BF), "tf": sb(S_, BF), "ya": sb(NY, F32), "yd": sb(NY, F32), "ys": sb(240, U16),
+    "ytf": sb(128, U16), "offf": sb(64, U16),
+    "la": sb(NB, F32), "lb": sb(NB, F32), "wa": sb(NB, F32), "ma": sb(NB, F32),
     "res0": sb(ZC + 8, F32), "res1": sb(ZC + 8, F32), "yt_0": sb(S_, F32), "yt_1": sb(S_, F32),
     "ps": ("psum", [128, 4096], F32),
 }
-SEMAPHORES = ["sv", "sa", "st", "sg", "dml", "dm2", "xl0", "xl1", "wl", "vps", "yst",
-              "aDM", "aS0", "aSL", "aCNT", "aE", "aL", "loc"]
+SEMAPHORES = ["sv", "sa", "st", "sg", "dml", "dm2", "xl0", "xl1", "wl", "xw", "vps", "yst",
+              "aDM", "aS0", "aD", "aSL", "aCNT", "aE", "aL", "loc"]
 
 
 def rank_program(g, core, T, topo):
@@ -59,7 +64,7 @@ def rank_program(g, core, T, topo):
     seen = {}
     L, U = slice(0, 64), slice(64, 128)
     QS = Q0, Q1, Q2, Q3 = tuple(slice(32 * k, 32 * k + 32) for k in range(4))
-    G0 = slice(0, 16)
+    G0, Q012 = slice(0, 16), slice(0, 96)
     even, local_first, fline = q < rp, q < rf, rf < rg
 
     def wait(name, eng, sem, n):
@@ -114,19 +119,33 @@ def rank_program(g, core, T, topo):
     def spread(off, c, src, d=0):
         return [tr(off[part, c:c + 32], src, d) for part in QS][-1]
 
+    def aline(out, in_, a, b, v=0, d=0):
+        return SA(lambda: g.scalar.activation(out, in_, AF.Identity, scale=a, bias=b), v, d)
+
     def iota(out, pattern, base, cm=0, whole=False):
         kw = {} if whole else {"allow_small_or_imprecise_dtypes": True}
         g.iota(out, pattern, base, cm, **kw).then_inc(s.sg, 1)
         cnt["sg"] += 1
         return cnt["sg"]
 
-    def send(dst, out, in_, rsem):
+    def send(dst, out, in_, rsem, en=None):
         rid, pid, _se = topo.addr(dst)
+        en = en or topo.engines(core, dst)
         g.remote_dma(out_ap=out, in_ap=in_, remote_sem=s[rsem], local_sem=s.loc, pid=pid, routing_id=rid,
-                     dma_engine_mask=topo.mask(core, dst))
-        cnt["loc"] += len(topo.engines(core, dst))
+                     dma_engine_mask=sum(1 << e for e in en))
+        cnt["loc"] += len(en)
+
+    def fused(writes):
+        trs = []
+        for dst, out, in_, rsem, en in writes:
+            rid, pid, _se = topo.addr(dst)
+            trs.append(RemoteDMATransfer(dst_ids=[DstId(rid=rid, pnc=pid)], dma_engine_mask=sum(1 << e for e in en),
+                                         remote_sem=s[rsem], src=in_, dst=out))
+            cnt["loc"] += len(en)
+        g.remote_dma_fused(trs, local_sem=s.loc)
 
     ncp, nmf = len(topo.engines(core, cp)), len(topo.engines(core, cf_))
+    ems = [e for e in topo.engines(core, cp) if e not in topo.engines(core, cf_)]
 
     def b8(ap):
         return ap.bitcast(dt.uint8)
@@ -144,9 +163,27 @@ def rank_program(g, core, T, topo):
         wait("g", g, "sa", n[1])
         send(dst, ls, ps_, rsem)
 
+    def stepper(gen):
+        last = [0]
+
+        def step(d=0):
+            vw("sv", max(last[0], d))
+            last[0] = next(gen) or last[0]
+            return last[0]
+        return step
+
     ob = 0 if even else 32
-    ndm2 = fill(T.dm2[:, ob:ob + 32], 0)
+    g.sync.dma_start(T.dmt[0:16, 4:36], T.dm[:, :]).then_inc(s.dml, 16)
+    g.scalar.dma_start(T.dmt[16:32, 3:35], T.dm[:, :]).then_inc(s.dml, 16)
+    for e, r in ((g.sync, 0), (g.scalar, 16)):
+        e.dma_start(T.dm2[r:r + 16, ob:ob + 32], T.dm[:, :]).then_inc(s.dm2, 16)
+    g.scalar.dma_start(T.xt[:, 1024:2048], T.x[:, 1024:2048]).then_inc(s.xl0, 16)
+    g.sync.dma_start(T.wt[:], T.w[:]).then_inc(s.wl, 16)
+    g.scalar.dma_start(T.xt[:, 0:1024], T.x[:, 0:1024]).then_inc(s.xl1, 16)
+
     fill(T.dmt[G0, 0:4], 0)
+    for part in (Q1, U):
+        ndm2 = fill(T.dm2[part, ob:ob + 32], 0)
     fill(T.winu[:, W0 + 1:2 * W0:2], 0.0)
     fill(T.one[:], 1.0)
     gpi = iota(T.pi[:, 0:1], [[1, 1]], 0, 1, whole=True)
@@ -157,156 +194,178 @@ def rank_program(g, core, T, topo):
         fill(T.eqv[part, :], float(c))
     for part, c in ((Q0, -2.0), (Q1, 2.0), (U, 2.0)):
         fill(T.sgn[part, :], c)
-    for j, c in enumerate((16.0, 1.0, 0.5, float(H))):
-        npf = ts(T.pf[:, j:j + 1], T.pint[:, j:j + 1], c, None, A.mult, d=n)
+    fill(T.k2[Q012, 0:1], 0.0)
+    fill(T.ct1[:, 31:64:32], 0.0)
+    for j, c in enumerate((16.0, 1.0, 0.5, S_ - 1.0)):
+        ts(T.pf[:, j:j + 1], T.pint[:, j:j + 1], c, None, A.mult, d=n)
+    npf = line(T.pf[:, 4:5], T.pint[:, 3:4], -2.0, 1.0)
     h256, s16 = T.pf[:, 0:1], T.pf[:, 1:2]
     for part, c in ((Q0, 2 * W0), (Q1, W0 - 2), (Q2, W0 - 2), (Q3, -2)):
         fill(T.ini[part, :], float(c))
-    fill(T.k2[0:96, 0:1], 0.0)
-    fill(T.two[Q0, :], 2.0)
-    ts(T.d0[:], T.one[:, 0:32], h256, None, A.is_gt, d=npf)
-    ts(T.k2[Q3, 0:1], T.pf[Q3, 0:1], 1.0 / 256, None, A.mult)
-    line(T.k2[:, 1:2], h256, -1.0, 256.0)
-    nk = ts(T.k2[:, 2:3], h256, -256.0, None, A.add)
-
-    g.sync.dma_start(T.dmt[0:16, 4:36], T.dm[:, :]).then_inc(s.dml, 16)
-    g.scalar.dma_start(T.dmt[16:32, 3:35], T.dm[:, :]).then_inc(s.dml, 16)
-    for name, e, r in (("s", g.sync, 0), ("a", g.scalar, 16)):
-        wait(name, e, "sv", ndm2)
-        e.dma_start(T.dm2[r:r + 16, ob:ob + 32], T.dm[:, :]).then_inc(s.dm2, 16)
-    g.scalar.dma_start(T.xt[:, 0:1024], T.x[:, 0:1024]).then_inc(s.xl0, 16)
-    g.sync.dma_start(T.xt[:, 1024:2048], T.x[:, 1024:2048]).then_inc(s.xl1, 16)
-    g.scalar.dma_start(T.wt[:], T.w[:]).then_inc(s.wl, 16)
 
     gdt = iota(T.dt0[:], [[0, 3], [16, 16]], DUMP)
-    gramp = iota(T.ramp[:], [[1, C]], -C)
+    gramp = iota(T.ramp[:], [[1, C]], -E)
     g.wait_ge(s.dm2, 32)
-    send(cp, T.dm2[:, ob:ob + 32], T.dm2[:, ob:ob + 32], "aDM")
+    wait("g", g, "sv", ndm2)
+    send(cp, T.dm2[:, ob:ob + 32], T.dm2[:, ob:ob + 32], "aDM", ems)
     gval = iota(T.val[:], [[1, 16], [16, 16]], 0)
     gi0 = iota(T.i0[Q0, :], [[16, NB]], 0)
-    ghm = iota(T.hm[:], [[0, 32]], 0)
 
     I, NI = T.ii[Q0, :], T.ni[Q0, :]
     g.vector.wait_ge(s.dml, 32)
     for part, m in ((Q0, G), (Q1, P | G), (Q2, Fb), (Q3, Fb)):
         n = ts(T.t1[part, :], T.dmt[Q0, 3:35], m, None, A.bitwise_and)
-    vw("sg", gdt)
-    ts(T.dtl[:], T.dt0[:], s16, None, A.add)
-    fill(T.yu[:], 0)
-    fill(T.z2[G0, 0:1], 0.0)
+    ts(T.d0[:], T.one[:, 0:32], h256, None, A.is_gt, d=npf)
+    ts(T.k2[Q3, 0:1], T.pf[Q3, 0:1], 1.0 / 256, None, A.mult)
+    line(T.k2[:, 1:2], h256, -1.0, 256.0)
+    nk = ts(T.k2[:, 2:3], h256, -256.0, None, A.add)
     n = ts(T.z1[:], T.t1[:], T.eqv[:], T.sgn[:], A.is_equal, A.mult, d=n)
     ts(T.x1[:, 32:64], T.t1[:], T.eqv[:], None, A.not_equal)
-    vw("sg", gramp)
-    ts(T.winu[:, W0:2 * W0:2], T.ramp[:], T.k2[:, 0:1], T.k2[:, 1:2], A.mult, A.add)
+    fill(T.yu[:], 0)
+    vw("sg", gdt)
+    ts(T.dtl[:], T.dt0[:], s16, None, A.add)
+    fill(T.two[Q0, :], 2.0)
+    kc = 1.0 if local_first else 0.5
+    fill(T.hs[Q0, :], -kc)
+    fill(T.hs[Q2, :], kc)
+    fill(T.z2[G0, 0:1], 0.0)
     n = scan(T.x1[:, 0:32], T.d0[:], T.z1[:], 0.0, n)
-    for j, c in enumerate((-BIG, 0.0, float(HOP - OWN - 256), 0.0, float(OWN + 256))):
-        fill(T.yd[Q0, j:5 * NB:5], c)
+    vw("sg", gramp)
+    line(T.winu[:, W0:2 * W0:2], T.ramp[:], T.k2[:, 0:1], T.k2[:, 1:2], nk)
+    fill(T.hm[Q0, 16:32], 0.0)
+    fill(T.msg[:], 0.0)
+    if not local_first:
+        fill(T.top[Q0, :], 2 * S_ + 1.0)
     n = tr(T.xt1[:], T.x1[:], n)
     g.vector.wait_ge(s.xl0, 16)
-    quant(T.xq, T.xs, T.xt, 0)
+    quant(T.xq, T.xs, T.xt, 256)
     scan(T.pt1[:], T.one[:, 0:32], T.xt1[:, 0:32], T.ini[:], n)
-    npt = tt(T.m1[:], T.xt1[:, 48:64], T.dtl[:, 0:16], A.mult)
-    quant(T.xq, T.xs, T.xt, 128)
-    tt(T.a1[Q0, 0:16], T.pt1[Q0, 16:32], T.m1[Q0, :], A.max, npt)
+    n = tt(T.m1[:], T.xt1[:, 48:64], T.dtl[:, 0:16], A.mult)
+    nxq = quant(T.xq, T.xs, T.xt, 384)
+    tt(T.a1[Q0, 0:16], T.pt1[Q0, 16:32], T.m1[Q0, :], A.max, n)
     n = tt(T.a1[Q0, 16:32], T.pt1[Q1, 16:32], T.m1[Q1, :], A.max)
+    line(T.rx1[Q0, 0:32], T.hs[Q0, :], T.pt1[Q0, 31:32], 2 * W0 * kc)
+    nrx = line(T.rx1[Q0, 32:64], T.hs[Q2, :], T.pt1[Q2, 31:32], (2 - W0) * kc)
     for part in (Q1, U):
         tt(T.o1[part, :], T.pt1[part, 16:32], T.m1[part, :], A.max)
-    for o_, c, i_ in ((L, 0, L), (U, 0, L), (L, 32, U), (U, 32, U)):
-        nrx = ts(T.rx1[o_, c:c + 32], T.one[i_, 0:32], T.pt1[i_, 31:32], None, A.mult)
     no1 = tt(T.o1[Q0, :], T.a1[Q0, 0:16], T.a1[Q0, 16:32], A.min, n)
-    g.vector.wait_ge(s.xl1, 16)
-    quant(T.xq, T.xs, T.xt, 256)
-    vw("sg", gval)
-    nwin = cpy(T.winu[:].indirect(T.o1[:]), T.val[:], no1)
-    nct = tr(T.ct1[:], T.rx1[:])
-    vw("sg", ghm)
-    nhm = ts(T.hm[Q0, 16:32], T.o1[Q0, :], -float(W0), 0.5, A.add, A.mult)
-    quant(T.xq, T.xs, T.xt, 384)
-
-    g.scalar.wait_ge(s.xl0, 16)
-    nwf = SA(lambda: g.scalar.activation(T.winf[:, 0:S_], T.xt[:, 0:S_], AF.Identity, scale=0.0, bias=-NONE))
-    wait("a", g.scalar, "sg", gval)
-    for part, c in ((L, 0), (U, 128)):
-        nvc = SA(lambda: g.scalar.activation(T.valc[part, :], T.val[part, c:c + 128], AF.Identity, bias=T.k2[part, 2:3]), nk)
-    wait("g", g, "sv", nct)
-    trs = []
-    for dst, land, h in ((cg_, T.cg, 0), (cf_, T.cf, 1)):
-        en = topo.engines(core, dst)
-        en = en[:len(en) // 2] if h == 0 else en[len(en) // 2:]
-        rid, pid, _se = topo.addr(dst)
-        trs.append(RemoteDMATransfer(dst_ids=[DstId(rid=rid, pnc=pid)], dma_engine_mask=sum(1 << e for e in en),
-                                     remote_sem=s.aCNT, src=T.ct1[:, 32 * h + 28:32 * h + 32], dst=land[:]))
-        cnt["loc"] += len(en)
-    g.remote_dma_fused(trs, local_sem=s.loc)
-
-    n = tr(T.tu[:], T.winu[:, W0:2 * W0], nwin)
-    nslu = tr(T.slu[:], T.hm[:], nhm)
-    g.vector.wait_ge(s.aDM, ncp)
-    g.vector.wait_ge(s.dm2, 32)
-    n2 = ts(T.t2[Q0, :], T.dm2[Q0, :], Qb, None, A.bitwise_and)
+    nct = tr(T.ct1[Q0, :], T.rx1[Q0, :], nrx)
     g.vector.wait_ge(s.wl, 16)
     quant(T.wq, T.ws, T.wt, 0)
-    tt(T.yu[:, 0:16], T.tu[:, 0:512:32], T.tu[:, 16:512:32], A.add, n)
-    n = tt(T.yu[:, 32:48], T.tu[:, 0:512:32], T.tu[:, 16:512:32], A.add)
+    vw("sg", gval)
+    nwin = cpy(T.winu[:].indirect(T.o1[:]), T.val[:], no1)
+    nhm = ts(T.hm[Q0, 0:16], T.o1[Q0, :], -float(W0), 0.5, A.add, A.mult)
+
+    g.scalar.wait_ge(s.xl0, 16)
+    aline(T.winf[:, 0:S_], T.xt[:, 1024:1024 + S_], 0.0, -NONE)
+    wait("a", g.scalar, "sg", gval)
+    for part, c in ((L, 0), (U, 128)):
+        nvc = aline(T.valc[part, :], T.val[part, c:c + 128], 1.0, T.k2[part, 2:3], nk)
+    n = aline(T.k2[Q0, 3:4], T.pf[Q0, 2:3], T.pf[Q0, 4:5], T.pf[Q0, 3:4])
+    aline(T.yd[Q0, 1:NY:2], T.xt[Q0, 1024:1024 + NY // 2], 0.0, 0.0)
+    wait("a", g.scalar, "sg", gi0)
+    n = aline(I, T.i0[Q0, :], T.pf[Q0, 4:5], T.k2[Q0, 3:4], 0, n)
+    for j, c in enumerate((-BIG, float(HOP - OWN - 256), float(OWN + 256))):
+        aline(T.yd[Q0, 2 * j:NY:6], T.xt[Q0, 1024:1024 + NB], 0.0, c)
+    nyd = aline(NI, I, -1.0, OWN - 1.0, 0, n)
+    res, yt = (T.res0, T.res1), (T.yt_0, T.yt_1)
+
+    def results(b, o):
+        base, width, pair, st = ((OWN + C, C, 0, 1), (OWN, C, 0, 3), (HOP, LT, 1, 5), (0, E, 2, 9), (E, C, 3, 11))[b]
+        a = 512 * (2 * pair + o)
+        wait("a", g.scalar, "st", st + o)
+        return SA(lambda: g.scalar.activation(res[o][:, base:base + width], T.ps[:, a:a + width], AF.Copy))
+    nhi = [results(0, o) for o in range(2)][-1]
+    wait("g", g, "sv", nct)
+    fused(((cg_, T.cg[:], T.ct1[:, 31:32], "aCNT", topo.engines(core, cg_)[:nmf // 2]),
+           (cf_, T.cf[:], T.ct1[:, 63:64], "aCNT", topo.engines(core, cf_)[nmf // 2:])))
+
+    u, v, nv = (T.sc[Q0, j:j + 1] for j in range(3))
+    u2, v2, tot = T.cf[Q0, :], T.cg[Q0, :], T.ct2[Q0, 31:32]
+    up, down = T.sc[Q0, 3:4], T.sc[Q0, 4:5]
+    if local_first:
+        u, v, up, down = u2, v2, -2.0, 2 * S_ + 1.0
+
+    def places():
+        g.vector.wait_ge(s.aDM, len(ems))
+        g.vector.wait_ge(s.dm2, 32)
+        yield ts(T.t2[Q0, :], T.dm2[Q0, :], Qb, None, A.bitwise_and)
+        ts(T.z2[G0, 1:65], T.t2[G0, :], 0.0, 2.0, A.is_gt, A.mult)
+        ts(T.x2[Q0, 64:128], T.t2[Q0, :], 0.0, None, A.is_equal)
+        yield ts(T.x2[Q0, 0:64], T.t2[Q0, :], 0.0, 2.0, A.is_gt, A.mult)
+        yield scan(T.x2[G0, 0:64], T.one[G0, :], T.z2[G0, 0:64], 0.0)
+        yield tr(T.xt2[Q0, :], T.x2[Q0, :])
+        if not local_first:
+            vw("aCNT", nmf)
+            ts(up, u2, v2, -2.0, A.add, A.add)
+            yield ts(down, T.top[Q0, :], u2, v2, A.subtract, A.subtract)
+        for c in (0, 32):
+            scan(T.pt2[Q0, c:c + 32], T.one[Q0, 0:32], T.xt2[Q0, c:c + 32], up)
+            n = scan(T.pr2[Q0, c:c + 32], T.one[Q0, 0:32], T.xt2[Q0, c:c + 32], down, op1=A.subtract)
+        tt(T.m2[Q0, :], T.xt2[Q0, 80:128], T.dtl[Q0, :], A.mult)
+        yield n
+        ts(T.rx2[Q0, :], T.two[Q0, :], T.pt2[Q0, 63:64], 0.5, A.add, A.mult)
+        yield tt(T.y2[Q0, :], T.pt2[Q0, 16:64], T.pr2[Q0, 16:64], A.min)
+        oc, pc = (0, 32) if even else (32, 0)
+        for part, c in ((Q0, oc), (Q1, pc), (Q2, oc + 8), (Q3, pc + 8)):
+            n = tt(T.o2[part, :], T.y2[Q0, c:c + 8], T.m2[Q0, c:c + 8], A.max)
+        yield n
+    place = stepper(places())
+
     nwq = quant(T.wq, T.ws, T.wt, 128)
-    n = tr(T.ytu[:], T.yu[:], n)
-    ts(T.z2[G0, 1:65], T.t2[G0, :], 0.0, 2.0, A.is_gt, A.mult, d=n2)
-    ts(T.x2[Q0, 64:128], T.t2[Q0, :], 0.0, None, A.is_equal)
-    n2 = ts(T.x2[Q0, 0:64], T.t2[Q0, :], 0.0, 2.0, A.is_gt, A.mult)
+    n = tr(T.tu[:], T.winu[:, W0:2 * W0], nwin)
+    nmsg = tr(T.msg[Q0, :], T.hm[Q0, :], nhm)
+    place()
+    g.vector.wait_ge(s.xl1, 16)
+    quant(T.xq, T.xs, T.xt, 0)
+    for part, o_, c in ((Q012, Q012, 0), (Q012, Q012, 32), (Q3, Q2, 16), (Q3, Q2, 48)):
+        nyu = tt(T.yu[o_, c:c + 16], T.tu[part, 0:512:32], T.tu[part, 16:512:32], A.add, n)
+    place()
+    n = tr(T.ytu[Q012, :], T.yu[Q012, :], nyu)
+    nxa = quant(T.xq, T.xs, T.xt, 128)
+    place()
     n0 = spread(T.off0, 0, T.ytu[Q0, 0:64:2], n)
     ne = spread(T.offe, 0, T.ytu[Q2, 0:64:2])
-    n2 = scan(T.x2[G0, 0:64], T.one[G0, :], T.z2[G0, 0:64], 0.0, n2)
-    p0 = pick(T.p0q[:], T.p0s[:], T.xq[:], T.xs[:], T.off0[:, 0:16], n0)
-    n2 = tr(T.xt2[Q0, :], T.x2[Q0, :], n2)
-    pe = pick(T.peq[:], T.pes[:], T.xq[:], T.xs[:], T.offe[:, 0:16], ne)
+    place()
+    p0 = pick(T.p0q[:, B:C], T.p0s[:, B:C], T.xq[:], T.xs[:], T.off0[:, 0:LT // 16], n0)
+    place()
+    pd = pick(T.p0q[:, 0:B], T.p0s[:, 0:B], T.xq[:], T.xs[:], T.off0[:, LT // 16:16], n0)
+    pe = pick(T.peq[:], T.pes[:], T.xq[:], T.xs[:], T.offe[:, 0:E // 16], ne)
+    for _ in range(2 if local_first else 3):
+        n2 = place()
 
-    wait("g", g, "sv", nslu)
-    send(cp, T.slin[:], T.slu[:], "aSL")
+    wait("g", g, "sv", nmsg)
+    send(cp, T.msi[:], T.msg[:], "aSL", ems)
     for b in (T.res0, T.res1):
         gz = iota(b[:, ZC:ZC + 8], [[0, 8]], 0)
-    send_pick(cp, T.xwq[:, 0:C], T.xws[:, 0:C], T.p0q[:], T.p0s[:], p0, "aS0")
+    send_pick(cp, T.xwq[:, 0:LT], T.xws[:, 0:LT], T.p0q[:, B:C], T.p0s[:, B:C], p0, "aS0")
+    wait("g", g, "sv", pd[0])
+    wait("g", g, "sa", pd[1])
+    fused(((cp, b8(T.plq[:, LT:C]), b8(T.p0q[:, 0:B]), "aD", ems[:len(ems) // 2]),
+           (cp, T.pls[:, LT:LT + 4 * B], T.p0s[:, 0:4 * B], "aD", ems[len(ems) // 2:])))
     send_pick(cf_, T.leq[:], T.les[:], T.peq[:], T.pes[:], pe, "aE")
-    g.sync.wait_ge(s.aSL, ncp)
+    wait("s", g.sync, "sv", nxq)
+    g.sync.dma_start(b8(T.xwq[:, E:T_]), b8(T.xq[:, E:T_])).then_inc(s.xw, 16)
+    g.sync.dma_start(T.xws[:, E:T_], T.xs[:, E:T_]).then_inc(s.xw, 16)
+    g.sync.wait_ge(s.aSL, len(ems))
     wait("s", g.sync, "sa", nvc)
     for k in range(4):
-        a, r, h = 32 + 64 * (k // 2) + 16 * (k % 2), 16 + 8 * (k // 2), 16 * (k % 2)
-        g.sync.dma_start(T.valc[a:a + 1, :], T.slin[r:r + 8, h:h + 16]).then_inc(s.vps, 16)
+        a, r, h = 32 + 64 * (k // 2) + 16 * (k % 2), 8 * (k // 2), 16 * (k % 2)
+        g.sync.dma_start(T.valc[a:a + 1, :], T.msi[r:r + 8, h:h + 16]).then_inc(s.vps, 16)
 
-    u, v, ini2, nv = (T.sc[Q0, j:j + 1] for j in range(4))
-    g.vector.wait_ge(s.aCNT, nmf)
-    n = n2
-    if local_first:
-        ini2 = -2.0
-    else:
-        n = ts(ini2, T.cf[Q0, 3:4], T.cg[Q0, 3:4], float(W0), A.subtract, A.add)
-    tt(T.m2[Q0, :], T.xt2[Q0, 80:128], T.dtl[Q0, :], A.mult, n2)
-    scan(T.pt2[Q0, 0:32], T.one[Q0, 0:32], T.xt2[Q0, 0:32], ini2, n)
-    n = scan(T.pt2[Q0, 32:64], T.one[Q0, 0:32], T.xt2[Q0, 32:64], ini2)
-    quant(T.xwq, T.xws, T.xt, C)
-    vw("sg", gi0)
-    nii = ts(I, T.i0[Q0, :], T.pf[Q0, 2:3], T.pf[Q0, 3:4], A.add, A.add)
-    nw = ts(T.w2[Q0, :], T.pt2[Q0, 16:64], float(S_), 1.0 - S_, A.is_ge, A.mult, d=n)
-    nrx = ts(T.rx2[Q0, :], T.two[Q0, :], T.pt2[Q0, 63:64], 0.5, A.add, A.mult)
-    quant(T.xwq, T.xws, T.xt, C + 128)
-    n = tt(T.y2[Q0, :], T.pt2[Q0, 16:64], T.w2[Q0, :], A.add, nw)
-    nxw = spread(T.offl, 0, T.ytu[Q3, 0:64:2])
-    tr(T.ct2[Q0, 0:32], T.rx2[Q0, :], nrx)
-    line(NI, I, -1.0, OWN - 1.0)
-    line(u, T.cf[Q0, 3:4], 0.5, 1.0 - C)
-    nc2 = line(v, T.cg[Q0, 3:4], -0.5, float(W0))
-    oc, pc = (0, 32) if even else (32, 0)
-    for part, c in ((Q0, oc), (Q1, pc), (Q2, oc + 8), (Q3, pc + 8)):
-        no2 = tt(T.o2[part, :], T.y2[Q0, c:c + 8], T.m2[Q0, c:c + 8], A.max, n)
-    fill(T.ys[Q0, :], 0)
-
-    tot = T.ct2[Q0, 31:32]
     if local_first:
         na_, nq, lnv = T.ct2[Q0, 32:33], T.ct2[Q0, 33:34], T.ct2[31:32, 32:34]
     else:
         na_, nq, lnv = tot, T.ct2[Q0, 32:33], T.ct2[31:32, 31:33]
-    la, lb, wa, wb, ma, mb = (t[Q0, :] for t in (T.la, T.lb, T.wa, T.wb, T.ma, T.mb))
+    la, lb, wa, ma = (t[Q0, :] for t in (T.la, T.lb, T.wa, T.ma))
+    mb, wb = T.ya[Q0, 4:NY:6], T.ya[Q0, 5:NY:6]
 
     def lines():
+        if not local_first:
+            ts(u, u2, 0.5, None, A.mult)
+            ts(v, v2, 0.5, None, A.mult)
+        yield tr(T.ct2[Q0, 0:32], T.rx2[Q0, :])
+        vw("aCNT", nmf)
         if local_first and fline:
             ts(la, I, tot, None, A.subtract)
             ts(lb, NI, u, tot, A.add, A.add)
@@ -324,83 +383,83 @@ def rank_program(g, core, T, topo):
             yield tt(ma, la, wa, A.add)
         else:
             ts(wa, I, u if fline else v, BIG if fline else -BIG, A.is_ge, A.mult)
-            yield ts(wb, I, na_, float(ZC), A.is_ge, A.mult)
             if fline:
                 ts(lb, NI, u, None, A.add)
             else:
                 ts(lb, I, v, OWN - 1.0, A.subtract, A.min)
+            yield ts(wb, I, na_, float(ZC), A.is_ge, A.mult)
             yield tt(ma, I if fline else NI, wa, A.add)
-            yield 0
         yield tt(mb, ma, lb, A.min if fline else A.max)
-        yield tt(T.ya[Q0, 4:5 * NB:5], mb, wb, A.max)
-    far = lines()
-    last = [nc2]
-
-    def step():
-        vw("sv", last[0])
-        last[0] = next(far) or last[0]
-
-    res, yt = (T.res0, T.res1), (T.yt_0, T.yt_1)
-
-    def results(b, o):
-        base, width = ((OWN, T_), (HOP, C), (0, C), (C, C))[b]
-        wait("a", g.scalar, "st", 2 * b + o + 1)
-        return SA(lambda: g.scalar.activation(res[o][:, base:base + width],
-                                              T.ps[:, 512 * (2 * b + o):512 * (2 * b + o) + width], AF.Copy))
+    step = stepper(lines())
     step()
-    results(0, 0)
-    results(0, 1)
-    g.vector.wait_ge(s.aS0, 2 * ncp)
-    g.scalar.wait_ge(s.aS0, 2 * ncp)
-    pl = pick(T.plq[:], T.pls[:], T.xwq[:], T.xws[:], T.offl[:, 0:16], nxw)
-    send_pick(cf_, T.llq[:], T.lls[:], T.plq[:], T.pls[:], pl, "aL")
 
-    step()
+    for o in range(2):
+        results(1, o)
+    for e in (g.vector, g.scalar):
+        e.wait_ge(s.xw, 32)
+        e.wait_ge(s.aS0, 2 * ncp)
+    pl = pick(T.plq[:, 0:LT], T.pls[:, 0:LT], T.xwq[:], T.xws[:], T.offe[:, E // 16:(E + LT) // 16], ne)
+    g.wait_ge(s.aD, len(ems))
+    send_pick(cf_, T.llq[:], T.lls[:], T.plq[:], T.pls[:, 0:C], pl, "aL")
+    for o in range(2):
+        results(2, o)
+
     g.vector.wait_ge(s.vps, 64)
-    vw("sa", nvc)
-    n = cpy(T.winf[:].indirect(T.o2[:]), T.valc[:], no2)
+    vw("sa", nyd)
+    n = cpy(T.winf[:].indirect(T.o2[:]), T.valc[:], n2)
     step()
-    n = tr(T.tf[:], T.winf[:, 0:S_], n)
+    tr(T.tf[:, 0:H], T.winf[:, 0:H], n)
     step()
+    n = tr(T.tf[:, H:S_], T.winf[:, H:S_])
+    step()
+    for c in (0, 48 + NY):
+        fill(T.ys[Q0, c:c + 48], 0)
     for j, part in enumerate((Q1, Q3, Q0, Q2)):
-        tt(T.ya[Q0, j:5 * NB:5], T.tf[part, 0:S_:32], T.tf[part, 16:S_:32], A.max, n)
-    step()
-    n = scan(T.ys[Q0, 0:5 * NB], T.yd[Q0, :], T.ya[Q0, :], 0.0, last[0], A.add, A.max)
+        nya = tt(T.ya[Q0, j:NY:6], T.tf[part, 0:S_:32], T.tf[part, 16:S_:32], A.max, n)
+        if local_first and j == 1:
+            step()
+    n = nya
+    n = scan(T.ys[Q0, 48:48 + NY], T.yd[Q0, :], T.ya[Q0, :], 0.0, n, A.add, A.max)
+    vw("st", 8)
+    for o in range(2):
+        cpy(res[o][:, HOP + LT:HOP + C], T.ps[:, 512 * o + 128 - B:512 * o + 128])
     if even:
-        nln = ts(nq, T.pt2[Q0, 31:32], ini2, 0.5, A.subtract, A.mult)
+        nln = ts(nq, T.pt2[Q0, 31:32], up, 0.5, A.subtract, A.mult)
     else:
         nln = ts(nq, T.pt2[Q0, 63:64], T.pt2[Q0, 31:32], 0.5, A.subtract, A.mult)
-    tr(T.ytf[Q0, 0:32], T.ys[Q0, 4:160:5], n)
-    n = tr(T.ytf[Q0, 32:64], T.ys[Q0, 4:160:5])
-    spread(T.offf, 0, T.ytf[Q0, 0:64:2], n)
-    noff = spread(T.offf, 32, T.ytf[Q0, 1:64:2])
+    tr(T.ytf[Q0, 0:32], T.ys[Q0, 53:240:6], n)
+    n = tr(T.ytf[Q0, 32:64], T.ys[Q0, 53:240:6])
+    for c in (64, 96):
+        nrev = tr(T.ytf[Q0, c:c + 32], T.ys[Q0, 191:4:-6])
+    noff = spread(T.offf, 0, T.ytf[Q0, 0:64:2], n)
 
     def mm(bank, o, qb, sbuf, a, n):
         g.tensor.matmul_mx(T.ps[:, 512 * bank:512 * bank + n], T.wq[:, 128 * o:128 * o + 128], T.ws[:, 128 * o:128 * o + 128],
                            qb[:, a:a + n], sbuf[:, a:a + n], True, True).then_inc(s.st, 1)
         cnt["st"] += 1
-    g.tensor.wait_ge(s.sv, nwq)
-    for bank, (qb, sbuf, n, sem, k) in enumerate(((T.xq, T.xs, T_, None, 0), (T.xwq, T.xws, C, "aS0", 2 * ncp),
-                                                  (T.leq, T.les, C, "aE", 2 * nmf), (T.llq, T.lls, C, "aL", 2 * nmf))):
-        if sem:
+    for pair, qb, sbuf, a, n, waits in ((0, T.xq, T.xs, C, C, (("sv", nwq),)), (0, T.xq, T.xs, 0, C, (("sv", nxa), ("sa", nhi))),
+                                        (1, T.xwq, T.xws, 0, LT, (("aS0", 2 * ncp),)),
+                                        (0, T.plq, T.pls, C - 128, 128, (("aD", len(ems)), ("sv", pl[0]), ("sa", pl[1]))),
+                                        (2, T.leq, T.les, 0, E, (("aE", 2 * nmf),)), (3, T.llq, T.lls, 0, C, (("aL", 2 * nmf),))):
+        for sem, k in waits:
             g.tensor.wait_ge(s[sem], k)
         for o in range(2):
-            mm(2 * bank + o, o, qb, sbuf, 0, n)
-    for b, o in ((1, 0), (1, 1), (2, 0), (2, 1)):
+            mm(2 * pair + o, o, qb, sbuf, a, n)
+    for b, o in ((3, 0), (3, 1), (4, 0)):
         nres0 = results(b, o)
-    ncop = results(3, 1)
-    vw("st", 7)
-    n0 = cpy(res[0][:, C:2 * C], T.ps[:, 512 * 6:512 * 6 + C])
+    n0 = noff
+    ncop = results(4, 1)
+    nhigh = spread(T.offf, 32, T.ytf[Q0, 127:64:-2], nrev)
 
     def window(o, a, b):
         c = a // 16 + (8 if a >= H else 0)
         return res[o][:].indirect(T.offf[:, c:c + (b - a) // 16])
 
     def vpick(o, a, b):
-        return cpy(yt[o][:, a:b], window(o, a, b), n0)
+        return cpy(yt[o][:, a:b], window(o, a, b), n0 if a < H else nhigh)
 
     def spick(o, a, b):
-        return SA(lambda: g.scalar.activation(yt[o][:, a:b], window(o, a, b), AF.Copy), noff, ncop)
+        return SA(lambda: g.scalar.activation(yt[o][:, a:b], window(o, a, b), AF.Copy), noff if a < H else nhigh, ncop)
 
     def store(o, a, b, v, a_=0):
         wait("s", g.sync, "sv", v)
@@ -412,13 +471,10 @@ def rank_program(g, core, T, topo):
     vw("sg", gz)
     wait("a", g.scalar, "sg", gz)
     vw("sa", nres0)
-    store(0, 0, 128, vpick(0, 0, 128))
-    store(0, 128, H, vpick(0, 128, H))
-    store(1, 0, 128, 0, spick(1, 0, 128))
-    store(1, 128, H, 0, spick(1, 128, H))
+    store(0, 0, 192, vpick(0, 0, 192))
+    store(0, 192, H, vpick(0, 192, H))
+    store(1, 0, H, 0, spick(1, 0, H))
     store(0, H, S_, vpick(0, H, S_))
-    n1 = spick(1, H, 640)
-    vw("sa", ncop)
-    store(1, H, S_, vpick(1, 640, S_), n1)
-    g.sync.wait_ge(s.yst, 16 * 7)
+    store(1, H, S_, 0, spick(1, H, S_))
+    g.sync.wait_ge(s.yst, 16 * 6)
     g.wait_ge(s.loc, cnt["loc"])

from concourse.bass import DstId, RemoteDMATransfer
from concourse.mybir import dt, AluOpType, ActivationFunctionType

T_, S_, C = 512, 768, 256
H = S_ // 2
NB = H // 16
NY = 6 * NB
W0 = 2 * C
DUMP = 2048
E, LT = 256, 224
B = C - LT
OWN, HOP, ZC = E + C, E + C + T_, E + 2 * C + T_
NONE = 4096.0
BIG = 8192.0

F32, I32, U16, BF = "float32", "int32", "uint16", "bfloat16"
Q4, U8 = "float8_e4m3fn_x4", "uint8"


def sb(n, d):
    return ("sbuf", [128, n], d)


SCRATCH = {
    "dmt": sb(36, I32), "dm2": sb(64, I32),
    "xt": sb(2048, BF), "wt": sb(1024, BF),
    "xq": sb(T_, Q4), "xs": sb(T_, U8), "wq": sb(256, Q4), "ws": sb(256, U8),
    "xwq": sb(T_, Q4), "xws": sb(T_, U8),
    "p0q": sb(C, Q4), "p0s": sb(C, U8), "peq": sb(E, Q4), "pes": sb(E, U8), "plq": sb(C, Q4), "pls": sb(LT + 4 * B, U8),
    "leq": sb(E, Q4), "les": sb(E, U8), "llq": sb(C, Q4), "lls": sb(C, U8),
    "pi": sb(2, I32), "pint": sb(4, I32), "pf": sb(6, F32), "one": sb(64, F32), "two": sb(32, F32), "hs": sb(32, F32), "d0": sb(32, F32),
    "eqv": sb(1, F32), "sgn": sb(1, F32), "ini": sb(1, F32), "k2": sb(4, F32), "dt0": sb(48, F32), "dtl": sb(48, F32),
    "val": sb(256, BF), "valc": sb(128, BF), "i0": sb(NB, F32), "ii": sb(NB, F32), "ni": sb(NB, F32),
    "t1": sb(32, I32), "z1": sb(32, F32), "x1": sb(64, F32), "xt1": sb(64, F32), "pt1": sb(32, F32), "m1": sb(16, F32),
    "a1": sb(32, F32), "o1": sb(16, U16), "ramp": sb(C, BF), "hm": sb(32, BF), "msg": sb(32, BF), "msi": sb(32, BF),
    "rx1": sb(64, F32), "ct1": sb(64, F32),
    "winu": sb(DUMP + 256, BF), "tu": sb(512, BF), "yu": sb(64, U16), "ytu": sb(64, U16),
    "off0": sb(32, U16), "offe": sb(32, U16),
    "cf": sb(1, F32), "cg": sb(1, F32), "sc": sb(8, F32),
    "t2": sb(64, I32), "z2": sb(66, BF), "x2": sb(128, BF), "xt2": sb(128, BF), "pt2": sb(64, F32),
    "pr2": sb(64, F32), "top": sb(1, F32), "m2": sb(48, F32),
    "w2": sb(48, F32), "y2": sb(48, F32), "o2": sb(8, U16), "rx2": sb(32, F32), "ct2": sb(40, F32),
    "winf": sb(DUMP + 256, BF), "tf": sb(S_, BF), "ya": sb(NY, F32), "yd": sb(NY, F32), "ys": sb(240, U16),
    "ytf": sb(128, U16), "offf": sb(64, U16),
    "la": sb(NB, F32), "lb": sb(NB, F32), "wa": sb(NB, F32), "ma": sb(NB, F32),
    "res0": sb(ZC + 8, F32), "res1": sb(ZC + 8, F32), "yt_0": sb(S_, F32), "yt_1": sb(S_, F32),
    "ps": ("psum", [128, 4096], F32),
}
SEMAPHORES = ["sv", "sa", "st", "sg", "dml", "dm2", "xl0", "xl1", "wl", "xw", "vps", "yst",
              "aDM", "aS0", "aD", "aSL", "aCNT", "aE", "aL", "loc"]


def rank_program(g, core, T, topo):
    q = T.rank_of(core)
    if q is None:
        return
    A = AluOpType
    AF = ActivationFunctionType
    rp, rf, rg = q ^ 1, q ^ 2, q ^ 3
    cp, cf_, cg_ = T.cores[rp], T.cores[rf], T.cores[rg]
    P, Fb, G, Qb = 1 << rp, 1 << rf, 1 << rg, 1 << q
    s = T.sem
    cnt = {"sv": 0, "sa": 0, "st": 0, "sg": 0, "loc": 0}
    seen = {}
    L, U = slice(0, 64), slice(64, 128)
    QS = Q0, Q1, Q2, Q3 = tuple(slice(32 * k, 32 * k + 32) for k in range(4))
    G0, Q012 = slice(0, 16), slice(0, 96)
    even, local_first, fline = q < rp, q < rf, rf < rg

    def wait(name, eng, sem, n):
        if n > 0 and seen.get((name, sem), 0) < n:
            seen[(name, sem)] = n
            eng.wait_ge(s[sem], n)

    def V(ins, d=0):
        wait("v", g.vector, "sv", d)
        r = ins()
        cnt["sv"] += 1
        r.then_inc(s.sv, 1)
        return cnt["sv"]

    def SA(ins, v=0, a=0):
        wait("a", g.scalar, "sv", v)
        wait("a", g.scalar, "sa", a)
        r = ins()
        cnt["sa"] += 1
        r.then_inc(s.sa, 1)
        return cnt["sa"]

    def vw(sem, n):
        wait("v", g.vector, sem, n)

    def ts(out, in0, s1, s2, op0, op1=None, d=0):
        if op1 is None:
            return V(lambda: g.vector.tensor_scalar(out, in0, s1, s2, op0), d)
        return V(lambda: g.vector.tensor_scalar(out, in0, s1, s2, op0, op1), d)

    def line(out, in0, a, b, d=0):
        return ts(out, in0, a, b, A.mult, A.add, d)

    def tt(out, a, b, op, d=0):
        return V(lambda: g.vector.tensor_tensor(out, a, b, op), d)

    def cpy(out, in_, d=0):
        return V(lambda: g.vector.tensor_copy(out, in_), d)

    def tr(out, in_, d=0):
        return V(lambda: g.vector.transpose(out, in_), d)

    def scan(out, d0, d1, init, d=0, op0=A.mult, op1=A.add):
        return V(lambda: g.vector.tensor_tensor_scan(out, d0, d1, init, op0, op1), d)

    def fill(ap, c, d=0):
        return V(lambda: g.vector.memset(ap, c), d)

    def quant(qb, sbuf, src, a):
        return V(lambda: g.vector.quantize_mx(qb[:, a:a + 128], sbuf[:, a:a + 128], src[:, 4 * a:4 * a + 512]))

    def spread(off, c, src, d=0):
        return [tr(off[part, c:c + 32], src, d) for part in QS][-1]

    def aline(out, in_, a, b, v=0, d=0):
        return SA(lambda: g.scalar.activation(out, in_, AF.Identity, scale=a, bias=b), v, d)

    def iota(out, pattern, base, cm=0, whole=False):
        kw = {} if whole else {"allow_small_or_imprecise_dtypes": True}
        g.iota(out, pattern, base, cm, **kw).then_inc(s.sg, 1)
        cnt["sg"] += 1
        return cnt["sg"]

    def send(dst, out, in_, rsem, en=None):
        rid, pid, _se = topo.addr(dst)
        en = en or topo.engines(core, dst)
        g.remote_dma(out_ap=out, in_ap=in_, remote_sem=s[rsem], local_sem=s.loc, pid=pid, routing_id=rid,
                     dma_engine_mask=sum(1 << e for e in en))
        cnt["loc"] += len(en)

    def fused(writes):
        trs = []
        for dst, out, in_, rsem, en in writes:
            rid, pid, _se = topo.addr(dst)
            trs.append(RemoteDMATransfer(dst_ids=[DstId(rid=rid, pnc=pid)], dma_engine_mask=sum(1 << e for e in en),
                                         remote_sem=s[rsem], src=in_, dst=out))
            cnt["loc"] += len(en)
        g.remote_dma_fused(trs, local_sem=s.loc)

    ncp, nmf = len(topo.engines(core, cp)), len(topo.engines(core, cf_))
    ems = [e for e in topo.engines(core, cp) if e not in topo.engines(core, cf_)]

    def b8(ap):
        return ap.bitcast(dt.uint8)

    def b32(ap):
        return ap.bitcast(dt.uint32)

    def pick(oq, os_, wq_, ws_, off, v):
        nq_ = cpy(b32(oq), b32(wq_).indirect(off), v)
        return nq_, SA(lambda: g.scalar.activation(os_, ws_.indirect(off), AF.Copy), v)

    def send_pick(dst, lq, ls, pq, ps_, n, rsem):
        wait("g", g, "sv", n[0])
        send(dst, b8(lq), b8(pq), rsem)
        wait("g", g, "sa", n[1])
        send(dst, ls, ps_, rsem)

    def stepper(gen):
        last = [0]

        def step(d=0):
            vw("sv", max(last[0], d))
            last[0] = next(gen) or last[0]
            return last[0]
        return step

    ob = 0 if even else 32
    g.sync.dma_start(T.dmt[0:16, 4:36], T.dm[:, :]).then_inc(s.dml, 16)
    g.scalar.dma_start(T.dmt[16:32, 3:35], T.dm[:, :]).then_inc(s.dml, 16)
    for e, r in ((g.sync, 0), (g.scalar, 16)):
        e.dma_start(T.dm2[r:r + 16, ob:ob + 32], T.dm[:, :]).then_inc(s.dm2, 16)
    g.scalar.dma_start(T.xt[:, 1024:2048], T.x[:, 1024:2048]).then_inc(s.xl0, 16)
    g.sync.dma_start(T.wt[:], T.w[:]).then_inc(s.wl, 16)
    g.scalar.dma_start(T.xt[:, 0:1024], T.x[:, 0:1024]).then_inc(s.xl1, 16)

    fill(T.dmt[G0, 0:4], 0)
    for part in (Q1, U):
        ndm2 = fill(T.dm2[part, ob:ob + 32], 0)
    fill(T.winu[:, W0 + 1:2 * W0:2], 0.0)
    fill(T.one[:], 1.0)
    gpi = iota(T.pi[:, 0:1], [[1, 1]], 0, 1, whole=True)
    vw("sg", gpi)
    for j, m in enumerate((16, 15, 30, 1)):
        n = ts(T.pint[:, j:j + 1], T.pi[:, 0:1], m, None, A.bitwise_and)
    for part, c in ((Q0, G), (Q1, P), (U, Fb)):
        fill(T.eqv[part, :], float(c))
    for part, c in ((Q0, -2.0), (Q1, 2.0), (U, 2.0)):
        fill(T.sgn[part, :], c)
    fill(T.k2[Q012, 0:1], 0.0)
    fill(T.ct1[:, 31:64:32], 0.0)
    for j, c in enumerate((16.0, 1.0, 0.5, S_ - 1.0)):
        ts(T.pf[:, j:j + 1], T.pint[:, j:j + 1], c, None, A.mult, d=n)
    npf = line(T.pf[:, 4:5], T.pint[:, 3:4], -2.0, 1.0)
    h256, s16 = T.pf[:, 0:1], T.pf[:, 1:2]
    for part, c in ((Q0, 2 * W0), (Q1, W0 - 2), (Q2, W0 - 2), (Q3, -2)):
        fill(T.ini[part, :], float(c))

    gdt = iota(T.dt0[:], [[0, 3], [16, 16]], DUMP)
    gramp = iota(T.ramp[:], [[1, C]], -E)
    g.wait_ge(s.dm2, 32)
    wait("g", g, "sv", ndm2)
    send(cp, T.dm2[:, ob:ob + 32], T.dm2[:, ob:ob + 32], "aDM", ems)
    gval = iota(T.val[:], [[1, 16], [16, 16]], 0)
    gi0 = iota(T.i0[Q0, :], [[16, NB]], 0)

    I, NI = T.ii[Q0, :], T.ni[Q0, :]
    g.vector.wait_ge(s.dml, 32)
    for part, m in ((Q0, G), (Q1, P | G), (Q2, Fb), (Q3, Fb)):
        n = ts(T.t1[part, :], T.dmt[Q0, 3:35], m, None, A.bitwise_and)
    ts(T.d0[:], T.one[:, 0:32], h256, None, A.is_gt, d=npf)
    ts(T.k2[Q3, 0:1], T.pf[Q3, 0:1], 1.0 / 256, None, A.mult)
    line(T.k2[:, 1:2], h256, -1.0, 256.0)
    nk = ts(T.k2[:, 2:3], h256, -256.0, None, A.add)
    n = ts(T.z1[:], T.t1[:], T.eqv[:], T.sgn[:], A.is_equal, A.mult, d=n)
    ts(T.x1[:, 32:64], T.t1[:], T.eqv[:], None, A.not_equal)
    fill(T.yu[:], 0)
    vw("sg", gdt)
    ts(T.dtl[:], T.dt0[:], s16, None, A.add)
    fill(T.two[Q0, :], 2.0)
    kc = 1.0 if local_first else 0.5
    fill(T.hs[Q0, :], -kc)
    fill(T.hs[Q2, :], kc)
    fill(T.z2[G0, 0:1], 0.0)
    n = scan(T.x1[:, 0:32], T.d0[:], T.z1[:], 0.0, n)
    vw("sg", gramp)
    line(T.winu[:, W0:2 * W0:2], T.ramp[:], T.k2[:, 0:1], T.k2[:, 1:2], nk)
    fill(T.hm[Q0, 16:32], 0.0)
    fill(T.msg[:], 0.0)
    if not local_first:
        fill(T.top[Q0, :], 2 * S_ + 1.0)
    n = tr(T.xt1[:], T.x1[:], n)
    g.vector.wait_ge(s.xl0, 16)
    quant(T.xq, T.xs, T.xt, 256)
    scan(T.pt1[:], T.one[:, 0:32], T.xt1[:, 0:32], T.ini[:], n)
    n = tt(T.m1[:], T.xt1[:, 48:64], T.dtl[:, 0:16], A.mult)
    nxq = quant(T.xq, T.xs, T.xt, 384)
    tt(T.a1[Q0, 0:16], T.pt1[Q0, 16:32], T.m1[Q0, :], A.max, n)
    n = tt(T.a1[Q0, 16:32], T.pt1[Q1, 16:32], T.m1[Q1, :], A.max)
    line(T.rx1[Q0, 0:32], T.hs[Q0, :], T.pt1[Q0, 31:32], 2 * W0 * kc)
    nrx = line(T.rx1[Q0, 32:64], T.hs[Q2, :], T.pt1[Q2, 31:32], (2 - W0) * kc)
    for part in (Q1, U):
        tt(T.o1[part, :], T.pt1[part, 16:32], T.m1[part, :], A.max)
    no1 = tt(T.o1[Q0, :], T.a1[Q0, 0:16], T.a1[Q0, 16:32], A.min, n)
    nct = tr(T.ct1[Q0, :], T.rx1[Q0, :], nrx)
    g.vector.wait_ge(s.wl, 16)
    quant(T.wq, T.ws, T.wt, 0)
    vw("sg", gval)
    nwin = cpy(T.winu[:].indirect(T.o1[:]), T.val[:], no1)
    nhm = ts(T.hm[Q0, 0:16], T.o1[Q0, :], -float(W0), 0.5, A.add, A.mult)

    g.scalar.wait_ge(s.xl0, 16)
    aline(T.winf[:, 0:S_], T.xt[:, 1024:1024 + S_], 0.0, -NONE)
    wait("a", g.scalar, "sg", gval)
    for part, c in ((L, 0), (U, 128)):
        nvc = aline(T.valc[part, :], T.val[part, c:c + 128], 1.0, T.k2[part, 2:3], nk)
    n = aline(T.k2[Q0, 3:4], T.pf[Q0, 2:3], T.pf[Q0, 4:5], T.pf[Q0, 3:4])
    aline(T.yd[Q0, 1:NY:2], T.xt[Q0, 1024:1024 + NY // 2], 0.0, 0.0)
    wait("a", g.scalar, "sg", gi0)
    n = aline(I, T.i0[Q0, :], T.pf[Q0, 4:5], T.k2[Q0, 3:4], 0, n)
    for j, c in enumerate((-BIG, float(HOP - OWN - 256), float(OWN + 256))):
        aline(T.yd[Q0, 2 * j:NY:6], T.xt[Q0, 1024:1024 + NB], 0.0, c)
    nyd = aline(NI, I, -1.0, OWN - 1.0, 0, n)
    res, yt = (T.res0, T.res1), (T.yt_0, T.yt_1)

    def results(b, o):
        base, width, pair, st = ((OWN + C, C, 0, 1), (OWN, C, 0, 3), (HOP, LT, 1, 5), (0, E, 2, 9), (E, C, 3, 11))[b]
        a = 512 * (2 * pair + o)
        wait("a", g.scalar, "st", st + o)
        return SA(lambda: g.scalar.activation(res[o][:, base:base + width], T.ps[:, a:a + width], AF.Copy))
    nhi = [results(0, o) for o in range(2)][-1]
    wait("g", g, "sv", nct)
    fused(((cg_, T.cg[:], T.ct1[:, 31:32], "aCNT", topo.engines(core, cg_)[:nmf // 2]),
           (cf_, T.cf[:], T.ct1[:, 63:64], "aCNT", topo.engines(core, cf_)[nmf // 2:])))

    u, v, nv = (T.sc[Q0, j:j + 1] for j in range(3))
    u2, v2, tot = T.cf[Q0, :], T.cg[Q0, :], T.ct2[Q0, 31:32]
    up, down = T.sc[Q0, 3:4], T.sc[Q0, 4:5]
    if local_first:
        u, v, up, down = u2, v2, -2.0, 2 * S_ + 1.0

    def places():
        g.vector.wait_ge(s.aDM, len(ems))
        g.vector.wait_ge(s.dm2, 32)
        yield ts(T.t2[Q0, :], T.dm2[Q0, :], Qb, None, A.bitwise_and)
        ts(T.z2[G0, 1:65], T.t2[G0, :], 0.0, 2.0, A.is_gt, A.mult)
        ts(T.x2[Q0, 64:128], T.t2[Q0, :], 0.0, None, A.is_equal)
        yield ts(T.x2[Q0, 0:64], T.t2[Q0, :], 0.0, 2.0, A.is_gt, A.mult)
        yield scan(T.x2[G0, 0:64], T.one[G0, :], T.z2[G0, 0:64], 0.0)
        yield tr(T.xt2[Q0, :], T.x2[Q0, :])
        if not local_first:
            vw("aCNT", nmf)
            ts(up, u2, v2, -2.0, A.add, A.add)
            yield ts(down, T.top[Q0, :], u2, v2, A.subtract, A.subtract)
        for c in (0, 32):
            scan(T.pt2[Q0, c:c + 32], T.one[Q0, 0:32], T.xt2[Q0, c:c + 32], up)
            n = scan(T.pr2[Q0, c:c + 32], T.one[Q0, 0:32], T.xt2[Q0, c:c + 32], down, op1=A.subtract)
        tt(T.m2[Q0, :], T.xt2[Q0, 80:128], T.dtl[Q0, :], A.mult)
        yield n
        ts(T.rx2[Q0, :], T.two[Q0, :], T.pt2[Q0, 63:64], 0.5, A.add, A.mult)
        yield tt(T.y2[Q0, :], T.pt2[Q0, 16:64], T.pr2[Q0, 16:64], A.min)
        oc, pc = (0, 32) if even else (32, 0)
        for part, c in ((Q0, oc), (Q1, pc), (Q2, oc + 8), (Q3, pc + 8)):
            n = tt(T.o2[part, :], T.y2[Q0, c:c + 8], T.m2[Q0, c:c + 8], A.max)
        yield n
    place = stepper(places())

    nwq = quant(T.wq, T.ws, T.wt, 128)
    n = tr(T.tu[:], T.winu[:, W0:2 * W0], nwin)
    nmsg = tr(T.msg[Q0, :], T.hm[Q0, :], nhm)
    place()
    g.vector.wait_ge(s.xl1, 16)
    quant(T.xq, T.xs, T.xt, 0)
    for part, o_, c in ((Q012, Q012, 0), (Q012, Q012, 32), (Q3, Q2, 16), (Q3, Q2, 48)):
        nyu = tt(T.yu[o_, c:c + 16], T.tu[part, 0:512:32], T.tu[part, 16:512:32], A.add, n)
    place()
    n = tr(T.ytu[Q012, :], T.yu[Q012, :], nyu)
    nxa = quant(T.xq, T.xs, T.xt, 128)
    place()
    n0 = spread(T.off0, 0, T.ytu[Q0, 0:64:2], n)
    ne = spread(T.offe, 0, T.ytu[Q2, 0:64:2])
    place()
    p0 = pick(T.p0q[:, B:C], T.p0s[:, B:C], T.xq[:], T.xs[:], T.off0[:, 0:LT // 16], n0)
    place()
    pd = pick(T.p0q[:, 0:B], T.p0s[:, 0:B], T.xq[:], T.xs[:], T.off0[:, LT // 16:16], n0)
    pe = pick(T.peq[:], T.pes[:], T.xq[:], T.xs[:], T.offe[:, 0:E // 16], ne)
    for _ in range(2 if local_first else 3):
        n2 = place()

    wait("g", g, "sv", nmsg)
    send(cp, T.msi[:], T.msg[:], "aSL", ems)
    for b in (T.res0, T.res1):
        gz = iota(b[:, ZC:ZC + 8], [[0, 8]], 0)
    send_pick(cp, T.xwq[:, 0:LT], T.xws[:, 0:LT], T.p0q[:, B:C], T.p0s[:, B:C], p0, "aS0")
    wait("g", g, "sv", pd[0])
    wait("g", g, "sa", pd[1])
    fused(((cp, b8(T.plq[:, LT:C]), b8(T.p0q[:, 0:B]), "aD", ems[:len(ems) // 2]),
           (cp, T.pls[:, LT:LT + 4 * B], T.p0s[:, 0:4 * B], "aD", ems[len(ems) // 2:])))
    send_pick(cf_, T.leq[:], T.les[:], T.peq[:], T.pes[:], pe, "aE")
    wait("s", g.sync, "sv", nxq)
    g.sync.dma_start(b8(T.xwq[:, E:T_]), b8(T.xq[:, E:T_])).then_inc(s.xw, 16)
    g.sync.dma_start(T.xws[:, E:T_], T.xs[:, E:T_]).then_inc(s.xw, 16)
    g.sync.wait_ge(s.aSL, len(ems))
    wait("s", g.sync, "sa", nvc)
    for k in range(4):
        a, r, h = 32 + 64 * (k // 2) + 16 * (k % 2), 8 * (k // 2), 16 * (k % 2)
        g.sync.dma_start(T.valc[a:a + 1, :], T.msi[r:r + 8, h:h + 16]).then_inc(s.vps, 16)

    if local_first:
        na_, nq, lnv = T.ct2[Q0, 32:33], T.ct2[Q0, 33:34], T.ct2[31:32, 32:34]
    else:
        na_, nq, lnv = tot, T.ct2[Q0, 32:33], T.ct2[31:32, 31:33]
    la, lb, wa, ma = (t[Q0, :] for t in (T.la, T.lb, T.wa, T.ma))
    mb, wb = T.ya[Q0, 4:NY:6], T.ya[Q0, 5:NY:6]

    def lines():
        if not local_first:
            ts(u, u2, 0.5, None, A.mult)
            ts(v, v2, 0.5, None, A.mult)
        yield tr(T.ct2[Q0, 0:32], T.rx2[Q0, :])
        vw("aCNT", nmf)
        if local_first and fline:
            ts(la, I, tot, None, A.subtract)
            ts(lb, NI, u, tot, A.add, A.add)
            yield ts(na_, u, v, tot, A.add, A.add)
            ts(wa, la, u, BIG, A.is_ge, A.mult)
            yield ts(wb, I, na_, float(ZC), A.is_ge, A.mult)
            yield tt(ma, la, wa, A.add)
        elif local_first:
            ts(la, NI, tot, OWN - 1.0, A.add, A.min)
            ts(na_, u, v, tot, A.add, A.add)
            yield ts(nv, tot, v, None, A.add)
            ts(wa, I, nv, -BIG, A.is_ge, A.mult)
            ts(lb, I, nv, None, A.subtract)
            yield ts(wb, I, na_, float(ZC), A.is_ge, A.mult)
            yield tt(ma, la, wa, A.add)
        else:
            ts(wa, I, u if fline else v, BIG if fline else -BIG, A.is_ge, A.mult)
            if fline:
                ts(lb, NI, u, None, A.add)
            else:
                ts(lb, I, v, OWN - 1.0, A.subtract, A.min)
            yield ts(wb, I, na_, float(ZC), A.is_ge, A.mult)
            yield tt(ma, I if fline else NI, wa, A.add)
        yield tt(mb, ma, lb, A.min if fline else A.max)
    step = stepper(lines())
    step()

    for o in range(2):
        results(1, o)
    for e in (g.vector, g.scalar):
        e.wait_ge(s.xw, 32)
        e.wait_ge(s.aS0, 2 * ncp)
    pl = pick(T.plq[:, 0:LT], T.pls[:, 0:LT], T.xwq[:], T.xws[:], T.offe[:, E // 16:(E + LT) // 16], ne)
    g.wait_ge(s.aD, len(ems))
    send_pick(cf_, T.llq[:], T.lls[:], T.plq[:], T.pls[:, 0:C], pl, "aL")
    for o in range(2):
        results(2, o)

    g.vector.wait_ge(s.vps, 64)
    vw("sa", nyd)
    n = cpy(T.winf[:].indirect(T.o2[:]), T.valc[:], n2)
    step()
    tr(T.tf[:, 0:H], T.winf[:, 0:H], n)
    step()
    n = tr(T.tf[:, H:S_], T.winf[:, H:S_])
    step()
    for c in (0, 48 + NY):
        fill(T.ys[Q0, c:c + 48], 0)
    for j, part in enumerate((Q1, Q3, Q0, Q2)):
        nya = tt(T.ya[Q0, j:NY:6], T.tf[part, 0:S_:32], T.tf[part, 16:S_:32], A.max, n)
        if local_first and j == 1:
            step()
    n = nya
    n = scan(T.ys[Q0, 48:48 + NY], T.yd[Q0, :], T.ya[Q0, :], 0.0, n, A.add, A.max)
    vw("st", 8)
    for o in range(2):
        cpy(res[o][:, HOP + LT:HOP + C], T.ps[:, 512 * o + 128 - B:512 * o + 128])
    if even:
        nln = ts(nq, T.pt2[Q0, 31:32], up, 0.5, A.subtract, A.mult)
    else:
        nln = ts(nq, T.pt2[Q0, 63:64], T.pt2[Q0, 31:32], 0.5, A.subtract, A.mult)
    tr(T.ytf[Q0, 0:32], T.ys[Q0, 53:240:6], n)
    n = tr(T.ytf[Q0, 32:64], T.ys[Q0, 53:240:6])
    for c in (64, 96):
        nrev = tr(T.ytf[Q0, c:c + 32], T.ys[Q0, 191:4:-6])
    noff = spread(T.offf, 0, T.ytf[Q0, 0:64:2], n)

    def mm(bank, o, qb, sbuf, a, n):
        g.tensor.matmul_mx(T.ps[:, 512 * bank:512 * bank + n], T.wq[:, 128 * o:128 * o + 128], T.ws[:, 128 * o:128 * o + 128],
                           qb[:, a:a + n], sbuf[:, a:a + n], True, True).then_inc(s.st, 1)
        cnt["st"] += 1
    for pair, qb, sbuf, a, n, waits in ((0, T.xq, T.xs, C, C, (("sv", nwq),)), (0, T.xq, T.xs, 0, C, (("sv", nxa), ("sa", nhi))),
                                        (1, T.xwq, T.xws, 0, LT, (("aS0", 2 * ncp),)),
                                        (0, T.plq, T.pls, C - 128, 128, (("aD", len(ems)), ("sv", pl[0]), ("sa", pl[1]))),
                                        (2, T.leq, T.les, 0, E, (("aE", 2 * nmf),)), (3, T.llq, T.lls, 0, C, (("aL", 2 * nmf),))):
        for sem, k in waits:
            g.tensor.wait_ge(s[sem], k)
        for o in range(2):
            mm(2 * pair + o, o, qb, sbuf, a, n)
    for b, o in ((3, 0), (3, 1), (4, 0)):
        nres0 = results(b, o)
    n0 = noff
    ncop = results(4, 1)
    nhigh = spread(T.offf, 32, T.ytf[Q0, 127:64:-2], nrev)

    def window(o, a, b):
        c = a // 16 + (8 if a >= H else 0)
        return res[o][:].indirect(T.offf[:, c:c + (b - a) // 16])

    def vpick(o, a, b):
        return cpy(yt[o][:, a:b], window(o, a, b), n0 if a < H else nhigh)

    def spick(o, a, b):
        return SA(lambda: g.scalar.activation(yt[o][:, a:b], window(o, a, b), AF.Copy), noff if a < H else nhigh, ncop)

    def store(o, a, b, v, a_=0):
        wait("s", g.sync, "sv", v)
        wait("s", g.sync, "sa", a_)
        g.sync.dma_start(T.y[:, S_ * o + a:S_ * o + b], yt[o][:, a:b]).then_inc(s.yst, 16)

    wait("s", g.sync, "sv", nln)
    g.sync.dma_start(T.ln[:, :], lnv).then_inc(s.yst, 16)
    vw("sg", gz)
    wait("a", g.scalar, "sg", gz)
    vw("sa", nres0)
    store(0, 0, 192, vpick(0, 0, 192))
    store(0, 192, H, vpick(0, 192, H))
    store(1, 0, H, 0, spick(1, 0, H))
    store(0, H, S_, vpick(0, H, S_))
    store(1, H, S_, 0, spick(1, H, S_))
    g.sync.wait_ge(s.yst, 16 * 6)
    g.wait_ge(s.loc, cnt["loc"])
